import numpy as np
import ml_dtypes


def mxq(x, axis, fmt="e4m3"):
    dtype, down = {"e4m3": (ml_dtypes.float8_e4m3fn, 7), "e5m2": (ml_dtypes.float8_e5m2, 14)}[fmt]
    v = np.moveaxis(np.asarray(x, np.float32).astype(ml_dtypes.bfloat16).astype(np.float64), axis, -1)
    blocks = v.reshape(v.shape[:-1] + (-1, 32))
    amax = np.abs(blocks).max(-1, keepdims=True)
    byte = np.maximum(np.where(amax > 0, np.frexp(amax)[1] - 1 + 127, 0) - down, 1)
    scale = np.exp2(byte - 127.0)
    codes = (blocks / scale).astype(np.float32).astype(dtype).astype(np.float64)
    return np.moveaxis((codes * scale).reshape(v.shape), -1, axis)


WIDE = False


def mx_kscale(k):
    if not WIDE:
        return np.ones(k)
    levels = np.array([10, -10, 5, -5, 0])
    if k % 512:
        return np.exp2(np.random.permutation(np.resize(levels, k // 32))).repeat(32)
    a = np.empty((k // 512, 16))
    for p in range(k // 512):
        a[p, :8] = np.random.permutation(np.resize(levels, 8))
        for g in range(8):
            far = levels[np.abs(levels - a[p, g]) >= 10]
            a[p, g + 8] = far[np.random.randint(len(far))]
    return np.exp2(a.ravel()).repeat(32)


def f64(x):
    return np.asarray(x).astype(np.float64)


def striped(idx):
    return np.tile(np.asarray(idx).reshape(-1, 16).T, (8, 1)).astype(np.uint16)


def unstriped(offs):
    return offs[:16].T.reshape(-1).astype(np.int64)

def bf(x):
    return np.asarray(x, np.float32).astype(ml_dtypes.bfloat16)


def planes(Y):
    r, m = Y.shape
    b = f64(bf(Y)).reshape(r // 32, 32, m)
    amax = np.abs(b).max(1)
    byte = np.clip(np.where(amax > 0, np.frexp(amax)[1] - 1 + 127 - 7, 1), 1, 254)
    codes = (b * np.exp2(127.0 - byte)[:, None, :]).reshape(r, m).astype(np.float32).astype(ml_dtypes.float8_e4m3fn).view(np.uint8)
    words = codes.reshape(r // 512, 128, 4, m).transpose(0, 1, 3, 2)
    return np.ascontiguousarray(words), np.ascontiguousarray(byte.astype(np.uint8).reshape(r // 512, 16, m))


B, N, T, D, NQ = 1, 512, 2048, 512, 512
DV = 512


def setup_inputs():
    n = np.random.standard_normal
    idx = np.sort(np.random.permutation(T)[:B * N].reshape(B, N), axis=1).reshape(-1)
    u = mx_kscale(N)
    ut = np.ones(T)
    ut[idx] = u
    return {
        "vT": (n((DV, T)) / ut).astype(np.float32),
        "wT": (np.random.dirichlet(np.ones(N), NQ).T[None] * u[:, None] * 16).astype(np.float32),
        "rs": (n((B, DV, NQ))).astype(np.float32),
        "offs": striped(idx),
    }


def reference(vT, wT, rs, offs):
    idx = unstriped(offs)
    pick = lambda x, which: x[:, which].reshape(x.shape[0], B, -1).transpose(1, 0, 2)
    wq = mxq(f64(wT), 1, "e4m3")
    o = mxq(pick(f64(vT), idx).transpose(0, 2, 1), 1, "e4m3").transpose(0, 2, 1) @ wq
    r_ = o + f64(rs)
    Y = r_[0]
    words, scales = planes(Y)
    return Y, words, scales

@@ -1,0 +1,142 @@
+from contextlib import ExitStack
+
+import concourse.mybir as mybir
+from concourse.masks import make_identity
+
+F32 = mybir.dt.float32
+BF16 = mybir.dt.bfloat16
+I32 = mybir.dt.int32
+U32 = mybir.dt.uint32
+U16 = mybir.dt.uint16
+U8 = mybir.dt.uint8
+FP8X4 = mybir.dt.float8_e4m3fn_x4
+ADD = mybir.AluOpType.add
+
+P = 128
+PACK = 4
+SLOTS = 512
+TOKENS = 2048
+NQ = 512
+HALF = NQ // 2
+FLOPS = 2 * 512 * 512 * 512
+
+
+def tile_attend_plo_wsumres_f_srt_kernel(tc, vT, wT, rs, offs, out_0, out_1, out_2):
+    nc = tc.nc
+    v_rows = vT.rearrange("(m u) t -> m u t", u=PACK)
+    w_rows = wT[0].rearrange("(p j) q -> p j q", j=PACK)
+    rs_rows = rs[0].rearrange("(m u) q -> m u q", u=PACK)
+    y_rows = out_0.rearrange("(m u) q -> m u q", u=PACK)
+    words_out = out_1[0].rearrange("p q u -> p (q u)").bitcast(I32)
+    scales_out = out_2[0].bitcast(I32)
+
+    with ExitStack() as ctx:
+        keep = ctx.enter_context(tc.tile_pool(name="keep", bufs=1))
+        psum = ctx.enter_context(tc.psum_pool(name="psum", bufs=1))
+
+        offsets = keep.tile([P, SLOTS // 16], U16, name="offsets")
+        v_raw = [keep.tile([P, TOKENS], F32, name="v_raw%d" % u, tag="v_raw%d" % u) for u in range(PACK)]
+        w_raw = keep.tile([P, PACK, NQ], F32, name="w_raw")
+        rs_sb = [keep.tile([P, NQ], F32, name="rs%d" % u) for u in range(PACK)]
+
+        nc.sync.dma_start(out=v_raw[0][:], in_=v_rows[:, 0, :])
+        nc.sync.dma_start(offsets[:], offs)
+        nc.sync.dma_start(out=w_raw[:], in_=w_rows)
+        for u in range(1, PACK):
+            nc.sync.dma_start(out=v_raw[u][:], in_=v_rows[:, u, :])
+        for u in range(PACK):
+            nc.sync.dma_start(out=rs_sb[u][:], in_=rs_rows[:, u, :])
+
+        identity = keep.tile([P, P], F32, name="identity")
+        make_identity(nc, identity[:])
+
+        w_grouped = keep.tile([P, NQ, PACK], BF16, name="w_grouped", align_bytes=64)
+        w_codes = keep.tile([P, NQ], U32, name="w_codes", align_bytes=64)
+        w_scales = keep.tile([P, NQ], U8, name="w_scales", align_bytes=64)
+        y_grouped = keep.tile([P, NQ, PACK], BF16, name="y_grouped", align_bytes=64)
+        y_codes = keep.tile([P, NQ], U32, name="y_codes", align_bytes=64)
+        y_scales = keep.tile([P, NQ], U8, name="y_scales", align_bytes=64)
+
+        def quantise_values(u):
+            gathered = keep.tile([P, SLOTS], BF16, name="gathered%d" % u, align_bytes=64)
+            nc.vector.tensor_copy(gathered[:], v_raw[u][:].indirect(offsets[:]))
+            pairs = gathered[:].bitcast(F32)
+            turned = psum.tile([P, 2, P], F32, name="turned%d" % (u % 2))
+            for h in range(2):
+                nc.tensor.transpose(turned[:, h, :], pairs[:, h : 2 * P : 2], identity[:])
+            grouped = keep.tile([P, P, PACK], BF16, name="v_grouped%d" % u, tag="v_grouped%d" % u, align_bytes=64)
+            nc.scalar.copy(out=grouped[:].bitcast(F32), in_=turned[:].rearrange("p h m -> p m h"))
+            codes = keep.tile([P, P], U32, name="v_codes%d" % u, align_bytes=64)
+            scales = keep.tile([P, P], U8, name="v_scales%d" % u, align_bytes=64)
+            nc.vector.quantize_mx(
+                out=codes[:].bitcast(FP8X4), scales=scales[:], in_=grouped[:].rearrange("p m t -> p (m t)")
+            )
+            return codes, scales
+
+        def product(u, codes, scales, cols, tag):
+            width = cols.stop - cols.start
+            acc = psum.tile([P, width], F32, name=tag)
+            nc.tensor.matmul_mx(
+                out=acc[:],
+                lhsT=codes[:].bitcast(FP8X4),
+                lhsT_scale=scales[:],
+                rhs=w_codes[:, cols].bitcast(FP8X4),
+                rhs_scale=w_scales[:, cols],
+                start=True,
+                stop=True,
+            )
+            return acc
+
+        def add_and_store(u, acc, cols):
+            y_u = y_pairs[u // 2][:, u % 2, cols]
+            nc.vector.tensor_tensor(y_u, acc[:], rs_sb[u][:, cols], ADD)
+            nc.sync.dma_start(out=y_rows[:, u, cols], in_=y_u)
+
+        whole = slice(0, NQ)
+        halves = [slice(0, HALF), slice(HALF, NQ)]
+
+        v_mx = [quantise_values(0)]
+        nc.scalar.copy(
+            out=w_grouped[:].rearrange("p (c i) t -> p c t i", i=4),
+            in_=w_raw[:].rearrange("p t (c i) -> p c t i", i=4),
+        )
+        nc.vector.quantize_mx(
+            out=w_codes[:].bitcast(FP8X4), scales=w_scales[:], in_=w_grouped[:].rearrange("p q t -> p (q t)")
+        )
+        accs = [product(0, v_mx[0][0], v_mx[0][1], whole, "acc0")]
+        for u in range(1, PACK - 1):
+            v_mx.append(quantise_values(u))
+            accs.append(product(u, v_mx[u][0], v_mx[u][1], whole, "acc%d" % u))
+        last = PACK - 1
+        codes, scales = quantise_values(last)
+        last_accs = [product(last, codes, scales, cols, "acc_last%d" % i) for i, cols in enumerate(halves)]
+        y_pairs = [
+            keep.tile([P, 2, NQ], F32, name="y_low", tag="v_raw%d" % last),
+            keep.tile([P, 2, NQ], F32, name="y_high", tag="v_grouped%d" % last, align_bytes=64),
+        ]
+        for u in range(PACK - 1):
+            add_and_store(u, accs[u], whole)
+        nc.scalar.copy(
+            out=y_grouped[:, :, 0:2],
+            in_=y_pairs[0][:].rearrange("p u q -> p q u"),
+        )
+        for i, cols in enumerate(halves):
+            add_and_store(last, last_accs[i], cols)
+        for cols in halves:
+            nc.vector.tensor_copy(
+                out=y_grouped[:, cols, 2:4],
+                in_=y_pairs[1][:, :, cols].rearrange("p u q -> p q u"),
+            )
+        for cols in halves:
+            nc.vector.quantize_mx(
+                out=y_codes[:, cols].bitcast(FP8X4),
+                scales=y_scales[:, cols],
+                in_=y_grouped[:, cols, :].rearrange("p q u -> p (q u)"),
+            )
+            nc.sync.dma_start(out=words_out[:, cols], in_=y_codes[:, cols].bitcast(I32))
+        for quad in range(4):
+            queue = nc.scalar if quad % 2 == 0 else nc.sync
+            queue.dma_start(
+                out=scales_out[4 * quad : 4 * quad + 4, :],
+                in_=y_scales[32 * quad : 32 * quad + 4, :].bitcast(I32),
+            )

@@ -18,6 +18,7 @@ SLOTS = 512
 TOKENS = 2048
 NQ = 512
 HALF = NQ // 2
+W_SPLIT = 384
 FLOPS = 2 * 512 * 512 * 512
 
 
@@ -35,30 +36,32 @@ def tile_attend_plo_wsumres_f_srt_kernel(tc, vT, wT, rs, offs, out_0, out_1, out
         psum = ctx.enter_context(tc.psum_pool(name="psum", bufs=1))
 
         offsets = keep.tile([P, SLOTS // 16], U16, name="offsets")
-        v_raw = [keep.tile([P, TOKENS], F32, name="v_raw%d" % u, tag="v_raw%d" % u) for u in range(PACK)]
-        w_raw = keep.tile([P, PACK, NQ], F32, name="w_raw")
+        v_raw = [keep.tile([P, TOKENS], F32, name="v_raw%d" % u, tag="v_raw%d" % u, align_bytes=64) for u in range(PACK)]
+        w_raw = keep.tile([P, PACK, NQ], F32, name="w_raw", tag="w_raw", align_bytes=64)
         rs_sb = [keep.tile([P, NQ], F32, name="rs%d" % u) for u in range(PACK)]
 
         nc.sync.dma_start(out=v_raw[0][:], in_=v_rows[:, 0, :])
         nc.sync.dma_start(offsets[:], offs)
-        nc.sync.dma_start(out=w_raw[:], in_=w_rows)
-        for u in range(1, PACK):
+        last = PACK - 1
+        for u in range(1, last):
             nc.sync.dma_start(out=v_raw[u][:], in_=v_rows[:, u, :])
+        nc.sync.dma_start(out=w_raw[:], in_=w_rows)
+        nc.sync.dma_start(out=v_raw[last][:], in_=v_rows[:, last, :])
         for u in range(PACK):
             nc.sync.dma_start(out=rs_sb[u][:], in_=rs_rows[:, u, :])
 
         identity = keep.tile([P, P], F32, name="identity")
         make_identity(nc, identity[:])
 
-        w_grouped = keep.tile([P, NQ, PACK], BF16, name="w_grouped", align_bytes=64)
+        w_grouped = keep.tile([P, NQ, PACK], BF16, name="w_grouped", tag="gathered%d" % last, align_bytes=64)
         w_codes = keep.tile([P, NQ], U32, name="w_codes", align_bytes=64)
         w_scales = keep.tile([P, NQ], U8, name="w_scales", align_bytes=64)
         y_grouped = keep.tile([P, NQ, PACK], BF16, name="y_grouped", align_bytes=64)
         y_codes = keep.tile([P, NQ], U32, name="y_codes", align_bytes=64)
         y_scales = keep.tile([P, NQ], U8, name="y_scales", align_bytes=64)
 
-        def quantise_values(u):
-            gathered = keep.tile([P, SLOTS], BF16, name="gathered%d" % u, align_bytes=64)
+        def gather_and_turn(u):
+            gathered = keep.tile([P, SLOTS], BF16, name="gathered%d" % u, tag="gathered%d" % u, align_bytes=64)
             nc.vector.tensor_copy(gathered[:], v_raw[u][:].indirect(offsets[:]))
             pairs = gathered[:].bitcast(F32)
             turned = psum.tile([P, 2, P], F32, name="turned%d" % (u % 2))
@@ -66,7 +69,10 @@ def tile_attend_plo_wsumres_f_srt_kernel(tc, vT, wT, rs, offs, out_0, out_1, out
                 nc.tensor.transpose(turned[:, h, :], pairs[:, h : 2 * P : 2], identity[:])
             grouped = keep.tile([P, P, PACK], BF16, name="v_grouped%d" % u, tag="v_grouped%d" % u, align_bytes=64)
             nc.scalar.copy(out=grouped[:].bitcast(F32), in_=turned[:].rearrange("p h m -> p m h"))
-            codes = keep.tile([P, P], U32, name="v_codes%d" % u, align_bytes=64)
+            return grouped
+
+        def quantise_values(u, grouped, codes_tag):
+            codes = keep.tile([P, P], U32, name="v_codes%d" % u, tag=codes_tag, align_bytes=64)
             scales = keep.tile([P, P], U8, name="v_scales%d" % u, align_bytes=64)
             nc.vector.quantize_mx(
                 out=codes[:].bitcast(FP8X4), scales=scales[:], in_=grouped[:].rearrange("p m t -> p (m t)")
@@ -95,38 +101,44 @@ def tile_attend_plo_wsumres_f_srt_kernel(tc, vT, wT, rs, offs, out_0, out_1, out
         whole = slice(0, NQ)
         halves = [slice(0, HALF), slice(HALF, NQ)]
 
-        v_mx = [quantise_values(0)]
-        nc.scalar.copy(
-            out=w_grouped[:].rearrange("p (c i) t -> p c t i", i=4),
-            in_=w_raw[:].rearrange("p t (c i) -> p c t i", i=4),
-        )
+        v_grouped = [gather_and_turn(0), gather_and_turn(1)]
+        v_mx = [quantise_values(0, v_grouped[0], "v_raw1")]
+        v_grouped.append(gather_and_turn(2))
+        v_mx.append(quantise_values(1, v_grouped[1], "v_raw2"))
+        for cols, copy in ((slice(0, W_SPLIT), nc.vector.tensor_copy), (slice(W_SPLIT, NQ), nc.scalar.copy)):
+            copy(
+                out=w_grouped[:, cols, :].rearrange("p (c i) t -> p c t i", i=4),
+                in_=w_raw[:, :, cols].rearrange("p t (c i) -> p c t i", i=4),
+            )
+        v_mx.append(quantise_values(2, v_grouped[2], "w_raw"))
         nc.vector.quantize_mx(
             out=w_codes[:].bitcast(FP8X4), scales=w_scales[:], in_=w_grouped[:].rearrange("p q t -> p (q t)")
         )
-        accs = [product(0, v_mx[0][0], v_mx[0][1], whole, "acc0")]
-        for u in range(1, PACK - 1):
-            v_mx.append(quantise_values(u))
-            accs.append(product(u, v_mx[u][0], v_mx[u][1], whole, "acc%d" % u))
-        last = PACK - 1
-        codes, scales = quantise_values(last)
+        accs = [product(u, v_mx[u][0], v_mx[u][1], whole, "acc%d" % u) for u in range(last)]
+        codes, scales = quantise_values(last, gather_and_turn(last), "v_codes_last")
         last_accs = [product(last, codes, scales, cols, "acc_last%d" % i) for i, cols in enumerate(halves)]
         y_pairs = [
-            keep.tile([P, 2, NQ], F32, name="y_low", tag="v_raw%d" % last),
+            keep.tile([P, 2, NQ], F32, name="y_low", tag="v_raw%d" % last, align_bytes=64),
             keep.tile([P, 2, NQ], F32, name="y_high", tag="v_grouped%d" % last, align_bytes=64),
         ]
-        for u in range(PACK - 1):
-            add_and_store(u, accs[u], whole)
-        nc.scalar.copy(
-            out=y_grouped[:, :, 0:2],
-            in_=y_pairs[0][:].rearrange("p u q -> p q u"),
-        )
+
+        def round_pair(copy, pair, cols):
+            copy(
+                out=y_grouped[:, cols, 2 * pair : 2 * pair + 2],
+                in_=y_pairs[pair][:, :, cols].rearrange("p u q -> p q u"),
+            )
+
+        add_and_store(0, accs[0], whole)
+        add_and_store(1, accs[1], whole)
+        round_pair(nc.scalar.copy, 0, halves[0])
+        round_pair(nc.vector.tensor_copy, 0, halves[1])
+        add_and_store(2, accs[2], whole)
         for i, cols in enumerate(halves):
             add_and_store(last, last_accs[i], cols)
         for cols in halves:
-            nc.vector.tensor_copy(
-                out=y_grouped[:, cols, 2:4],
-                in_=y_pairs[1][:, :, cols].rearrange("p u q -> p q u"),
-            )
+            middle = cols.start + HALF // 2
+            round_pair(nc.vector.tensor_copy, 1, slice(cols.start, middle))
+            round_pair(nc.scalar.copy, 1, slice(middle, cols.stop))
         for cols in halves:
             nc.vector.quantize_mx(
                 out=y_codes[:, cols].bitcast(FP8X4),

@@ -18,7 +18,7 @@ SLOTS = 512
 TOKENS = 2048
 NQ = 512
 HALF = NQ // 2
-W_SPLIT = 384
+W_SPLIT = 320
 FLOPS = 2 * 512 * 512 * 512
 
 
@@ -38,7 +38,7 @@ def tile_attend_plo_wsumres_f_srt_kernel(tc, vT, wT, rs, offs, out_0, out_1, out
         offsets = keep.tile([P, SLOTS // 16], U16, name="offsets")
         v_raw = [keep.tile([P, TOKENS], F32, name="v_raw%d" % u, tag="v_raw%d" % u, align_bytes=64) for u in range(PACK)]
         w_raw = keep.tile([P, PACK, NQ], F32, name="w_raw", tag="w_raw", align_bytes=64)
-        rs_sb = [keep.tile([P, NQ], F32, name="rs%d" % u) for u in range(PACK)]
+        rs_sb = keep.tile([P, PACK, NQ], F32, name="rs_sb")
 
         nc.sync.dma_start(out=v_raw[0][:], in_=v_rows[:, 0, :])
         nc.sync.dma_start(offsets[:], offs)
@@ -47,8 +47,8 @@ def tile_attend_plo_wsumres_f_srt_kernel(tc, vT, wT, rs, offs, out_0, out_1, out
             nc.sync.dma_start(out=v_raw[u][:], in_=v_rows[:, u, :])
         nc.sync.dma_start(out=w_raw[:], in_=w_rows)
         nc.sync.dma_start(out=v_raw[last][:], in_=v_rows[:, last, :])
-        for u in range(PACK):
-            nc.sync.dma_start(out=rs_sb[u][:], in_=rs_rows[:, u, :])
+        for planes in (slice(0, 1), slice(1, 2), slice(2, 4)):
+            nc.sync.dma_start(out=rs_sb[:, planes, :], in_=rs_rows[:, planes, :])
 
         identity = keep.tile([P, P], F32, name="identity")
         make_identity(nc, identity[:])
@@ -56,7 +56,6 @@ def tile_attend_plo_wsumres_f_srt_kernel(tc, vT, wT, rs, offs, out_0, out_1, out
         w_grouped = keep.tile([P, NQ, PACK], BF16, name="w_grouped", tag="gathered%d" % last, align_bytes=64)
         w_codes = keep.tile([P, NQ], U32, name="w_codes", align_bytes=64)
         w_scales = keep.tile([P, NQ], U8, name="w_scales", align_bytes=64)
-        y_grouped = keep.tile([P, NQ, PACK], BF16, name="y_grouped", align_bytes=64)
         y_codes = keep.tile([P, NQ], U32, name="y_codes", align_bytes=64)
         y_scales = keep.tile([P, NQ], U8, name="y_scales", align_bytes=64)
 
@@ -79,11 +78,10 @@ def tile_attend_plo_wsumres_f_srt_kernel(tc, vT, wT, rs, offs, out_0, out_1, out
             )
             return codes, scales
 
-        def product(u, codes, scales, cols, tag):
-            width = cols.stop - cols.start
-            acc = psum.tile([P, width], F32, name=tag)
+        def product(acc, values, cols):
+            codes, scales = values
             nc.tensor.matmul_mx(
-                out=acc[:],
+                out=acc,
                 lhsT=codes[:].bitcast(FP8X4),
                 lhsT_scale=scales[:],
                 rhs=w_codes[:, cols].bitcast(FP8X4),
@@ -91,12 +89,21 @@ def tile_attend_plo_wsumres_f_srt_kernel(tc, vT, wT, rs, offs, out_0, out_1, out
                 start=True,
                 stop=True,
             )
-            return acc
 
-        def add_and_store(u, acc, cols):
-            y_u = y_pairs[u // 2][:, u % 2, cols]
-            nc.vector.tensor_tensor(y_u, acc[:], rs_sb[u][:, cols], ADD)
-            nc.sync.dma_start(out=y_rows[:, u, cols], in_=y_u)
+        def add_residual(u, acc, cols):
+            nc.vector.tensor_tensor(y_pairs[u // 2][:, u % 2, cols], acc, rs_sb[:, u, cols], ADD)
+
+        def round_weights(copy, cols):
+            copy(
+                out=w_grouped[:, cols, :].rearrange("p (c i) t -> p c t i", i=4),
+                in_=w_raw[:, :, cols].rearrange("p t (c i) -> p c t i", i=4),
+            )
+
+        def round_pair(copy, pair, cols):
+            copy(
+                out=y_grouped[:, cols, 2 * pair : 2 * pair + 2],
+                in_=y_pairs[pair][:, :, cols].rearrange("p u q -> p q u"),
+            )
 
         whole = slice(0, NQ)
         halves = [slice(0, HALF), slice(HALF, NQ)]
@@ -105,40 +112,39 @@ def tile_attend_plo_wsumres_f_srt_kernel(tc, vT, wT, rs, offs, out_0, out_1, out
         v_mx = [quantise_values(0, v_grouped[0], "v_raw1")]
         v_grouped.append(gather_and_turn(2))
         v_mx.append(quantise_values(1, v_grouped[1], "v_raw2"))
-        for cols, copy in ((slice(0, W_SPLIT), nc.vector.tensor_copy), (slice(W_SPLIT, NQ), nc.scalar.copy)):
-            copy(
-                out=w_grouped[:, cols, :].rearrange("p (c i) t -> p c t i", i=4),
-                in_=w_raw[:, :, cols].rearrange("p t (c i) -> p c t i", i=4),
-            )
-        v_mx.append(quantise_values(2, v_grouped[2], "w_raw"))
-        nc.vector.quantize_mx(
-            out=w_codes[:].bitcast(FP8X4), scales=w_scales[:], in_=w_grouped[:].rearrange("p q t -> p (q t)")
-        )
-        accs = [product(u, v_mx[u][0], v_mx[u][1], whole, "acc%d" % u) for u in range(last)]
-        codes, scales = quantise_values(last, gather_and_turn(last), "v_codes_last")
-        last_accs = [product(last, codes, scales, cols, "acc_last%d" % i) for i, cols in enumerate(halves)]
-        y_pairs = [
-            keep.tile([P, 2, NQ], F32, name="y_low", tag="v_raw%d" % last, align_bytes=64),
-            keep.tile([P, 2, NQ], F32, name="y_high", tag="v_grouped%d" % last, align_bytes=64),
-        ]
-
-        def round_pair(copy, pair, cols):
-            copy(
-                out=y_grouped[:, cols, 2 * pair : 2 * pair + 2],
-                in_=y_pairs[pair][:, :, cols].rearrange("p u q -> p q u"),
-            )
-
-        add_and_store(0, accs[0], whole)
-        add_and_store(1, accs[1], whole)
-        round_pair(nc.scalar.copy, 0, halves[0])
-        round_pair(nc.vector.tensor_copy, 0, halves[1])
-        add_and_store(2, accs[2], whole)
+        round_weights(nc.vector.tensor_copy, slice(0, W_SPLIT))
+        round_weights(nc.scalar.copy, slice(W_SPLIT, NQ))
         for i, cols in enumerate(halves):
-            add_and_store(last, last_accs[i], cols)
+            nc.vector.quantize_mx(
+                out=w_codes[:, cols].bitcast(FP8X4),
+                scales=w_scales[:, cols],
+                in_=w_grouped[:, cols, :].rearrange("p q t -> p (q t)"),
+            )
+            if i == 0:
+                v_mx.append(quantise_values(2, v_grouped[2], "w_raw"))
+        accs = [psum.tile([P, NQ], F32, name="acc%d" % u) for u in range(last)]
         for cols in halves:
-            middle = cols.start + HALF // 2
-            round_pair(nc.vector.tensor_copy, 1, slice(cols.start, middle))
-            round_pair(nc.scalar.copy, 1, slice(middle, cols.stop))
+            for u in range(last):
+                product(accs[u][:, cols], v_mx[u], cols)
+        v_grouped.append(gather_and_turn(last))
+        y_pairs = [keep.tile([P, 2, NQ], F32, name="y_low")]
+        y_grouped = keep.tile([P, NQ, PACK], BF16, name="y_grouped", tag="gathered%d" % last, align_bytes=64)
+        add_residual(0, accs[0][:], whole)
+        add_residual(1, accs[1][:], whole)
+        nc.sync.dma_start(out=y_rows[:, 0:2, :], in_=y_pairs[0][:])
+        round_pair(nc.scalar.copy, 0, whole)
+        v_mx.append(quantise_values(last, v_grouped[last], "v_codes_last"))
+        last_accs = [psum.tile([P, HALF], F32, name="acc_last%d" % i) for i in range(2)]
+        for acc, cols in zip(last_accs, halves):
+            product(acc[:], v_mx[last], cols)
+        y_pairs.append(keep.tile([P, 2, NQ], F32, name="y_high", tag="v_grouped%d" % last, align_bytes=64))
+        add_residual(2, accs[2][:], whole)
+        nc.sync.dma_start(out=y_rows[:, 2, :], in_=y_pairs[1][:, 0, :])
+        for acc, cols in zip(last_accs, halves):
+            add_residual(last, acc[:], cols)
+        nc.sync.dma_start(out=y_rows[:, last, :], in_=y_pairs[1][:, 1, :])
+        for cols in halves:
+            round_pair(nc.vector.tensor_copy, 1, cols)
         for cols in halves:
             nc.vector.quantize_mx(
                 out=y_codes[:, cols].bitcast(FP8X4),

@@ -18,6 +18,7 @@ SLOTS = 512
 TOKENS = 2048
 NQ = 512
 HALF = NQ // 2
+QUARTER = NQ // 4
 W_SPLIT = 320
 FLOPS = 2 * 512 * 512 * 512
 
@@ -114,25 +115,26 @@ def tile_attend_plo_wsumres_f_srt_kernel(tc, vT, wT, rs, offs, out_0, out_1, out
         v_mx.append(quantise_values(1, v_grouped[1], "v_raw2"))
         round_weights(nc.vector.tensor_copy, slice(0, W_SPLIT))
         round_weights(nc.scalar.copy, slice(W_SPLIT, NQ))
-        for i, cols in enumerate(halves):
+        for cols in halves:
             nc.vector.quantize_mx(
                 out=w_codes[:, cols].bitcast(FP8X4),
                 scales=w_scales[:, cols],
                 in_=w_grouped[:, cols, :].rearrange("p q t -> p (q t)"),
             )
-            if i == 0:
-                v_mx.append(quantise_values(2, v_grouped[2], "w_raw"))
+        v_mx.append(quantise_values(2, v_grouped[2], "w_raw"))
         accs = [psum.tile([P, NQ], F32, name="acc%d" % u) for u in range(last)]
-        for cols in halves:
-            for u in range(last):
-                product(accs[u][:, cols], v_mx[u], cols)
+        for planes in ((0, 1), (2,)):
+            for cols in halves:
+                for u in planes:
+                    product(accs[u][:, cols], v_mx[u], cols)
         v_grouped.append(gather_and_turn(last))
         y_pairs = [keep.tile([P, 2, NQ], F32, name="y_low")]
         y_grouped = keep.tile([P, NQ, PACK], BF16, name="y_grouped", tag="gathered%d" % last, align_bytes=64)
         add_residual(0, accs[0][:], whole)
         add_residual(1, accs[1][:], whole)
         nc.sync.dma_start(out=y_rows[:, 0:2, :], in_=y_pairs[0][:])
-        round_pair(nc.scalar.copy, 0, whole)
+        for cols in halves:
+            round_pair(nc.scalar.copy, 0, cols)
         v_mx.append(quantise_values(last, v_grouped[last], "v_codes_last"))
         last_accs = [psum.tile([P, HALF], F32, name="acc_last%d" % i) for i in range(2)]
         for acc, cols in zip(last_accs, halves):
@@ -143,8 +145,9 @@ def tile_attend_plo_wsumres_f_srt_kernel(tc, vT, wT, rs, offs, out_0, out_1, out
         for acc, cols in zip(last_accs, halves):
             add_residual(last, acc[:], cols)
         nc.sync.dma_start(out=y_rows[:, last, :], in_=y_pairs[1][:, 1, :])
-        for cols in halves:
-            round_pair(nc.vector.tensor_copy, 1, cols)
+        round_pair(nc.scalar.copy, 1, slice(0, QUARTER))
+        round_pair(nc.vector.tensor_copy, 1, slice(QUARTER, HALF))
+        round_pair(nc.vector.tensor_copy, 1, halves[1])
         for cols in halves:
             nc.vector.quantize_mx(
                 out=y_codes[:, cols].bitcast(FP8X4),

@@ -37,18 +37,18 @@ def tile_attend_plo_wsumres_f_srt_kernel(tc, vT, wT, rs, offs, out_0, out_1, out
         psum = ctx.enter_context(tc.psum_pool(name="psum", bufs=1))
 
         offsets = keep.tile([P, SLOTS // 16], U16, name="offsets")
-        v_raw = [keep.tile([P, TOKENS], F32, name="v_raw%d" % u, tag="v_raw%d" % u, align_bytes=64) for u in range(PACK)]
+        v_first = keep.tile([P, 2, TOKENS], F32, name="v_first", tag="v_raw1", align_bytes=64)
+        v_raw = {u: keep.tile([P, TOKENS], F32, name="v_raw%d" % u, tag="v_raw%d" % u, align_bytes=64) for u in (2, 3)}
         w_raw = keep.tile([P, PACK, NQ], F32, name="w_raw", tag="w_raw", align_bytes=64)
         rs_sb = keep.tile([P, PACK, NQ], F32, name="rs_sb")
 
-        nc.sync.dma_start(out=v_raw[0][:], in_=v_rows[:, 0, :])
+        nc.sync.dma_start(out=v_first[:], in_=v_rows[:, 0:2, :])
         nc.sync.dma_start(offsets[:], offs)
         last = PACK - 1
-        for u in range(1, last):
-            nc.sync.dma_start(out=v_raw[u][:], in_=v_rows[:, u, :])
+        nc.sync.dma_start(out=v_raw[2][:], in_=v_rows[:, 2, :])
         nc.sync.dma_start(out=w_raw[:], in_=w_rows)
         nc.sync.dma_start(out=v_raw[last][:], in_=v_rows[:, last, :])
-        for planes in (slice(0, 1), slice(1, 2), slice(2, 4)):
+        for planes in (slice(0, 2), slice(2, 4)):
             nc.sync.dma_start(out=rs_sb[:, planes, :], in_=rs_rows[:, planes, :])
 
         identity = keep.tile([P, P], F32, name="identity")
@@ -62,11 +62,18 @@ def tile_attend_plo_wsumres_f_srt_kernel(tc, vT, wT, rs, offs, out_0, out_1, out
 
         def gather_and_turn(u):
             gathered = keep.tile([P, SLOTS], BF16, name="gathered%d" % u, tag="gathered%d" % u, align_bytes=64)
-            nc.vector.tensor_copy(gathered[:], v_raw[u][:].indirect(offsets[:]))
             pairs = gathered[:].bitcast(F32)
+            if u == 1:
+                dealt = gathered[:].rearrange("p (h w e) -> p w h e", h=2, e=2)
+                nc.vector.tensor_copy(dealt, v_first[:, 1, :].indirect(offsets[:]))
+                words = [pairs[:, h * P : (h + 1) * P] for h in range(2)]
+            else:
+                window = v_first[:].rearrange("p u t -> p (u t)") if u == 0 else v_raw[u][:]
+                nc.vector.tensor_copy(gathered[:], window.indirect(offsets[:]))
+                words = [pairs[:, h : 2 * P : 2] for h in range(2)]
             turned = psum.tile([P, 2, P], F32, name="turned%d" % (u % 2))
             for h in range(2):
-                nc.tensor.transpose(turned[:, h, :], pairs[:, h : 2 * P : 2], identity[:])
+                nc.tensor.transpose(turned[:, h, :], words[h], identity[:])
             grouped = keep.tile([P, P, PACK], BF16, name="v_grouped%d" % u, tag="v_grouped%d" % u, align_bytes=64)
             nc.scalar.copy(out=grouped[:].bitcast(F32), in_=turned[:].rearrange("p h m -> p m h"))
             return grouped
@@ -127,22 +134,26 @@ def tile_attend_plo_wsumres_f_srt_kernel(tc, vT, wT, rs, offs, out_0, out_1, out
             for cols in halves:
                 for u in planes:
                     product(accs[u][:, cols], v_mx[u], cols)
+        acc0_low = keep.tile([P, HALF], F32, name="acc0_low")
+        nc.scalar.copy(out=acc0_low[:], in_=accs[0][:, halves[0]])
         v_grouped.append(gather_and_turn(last))
         y_pairs = [keep.tile([P, 2, NQ], F32, name="y_low")]
         y_grouped = keep.tile([P, NQ, PACK], BF16, name="y_grouped", tag="gathered%d" % last, align_bytes=64)
-        add_residual(0, accs[0][:], whole)
+        nc.gpsimd.tensor_tensor(y_pairs[0][:, 0, halves[0]], acc0_low[:], rs_sb[:, 0, halves[0]], ADD)
+        add_residual(0, accs[0][:, halves[1]], halves[1])
         add_residual(1, accs[1][:], whole)
         nc.sync.dma_start(out=y_rows[:, 0:2, :], in_=y_pairs[0][:])
         for cols in halves:
             round_pair(nc.scalar.copy, 0, cols)
         v_mx.append(quantise_values(last, v_grouped[last], "v_codes_last"))
-        last_accs = [psum.tile([P, HALF], F32, name="acc_last%d" % i) for i in range(2)]
-        for acc, cols in zip(last_accs, halves):
+        pieces = [slice(0, QUARTER), slice(QUARTER, HALF), halves[1]]
+        last_accs = [psum.tile([P, c.stop - c.start], F32, name="acc_last%d" % i) for i, c in enumerate(pieces)]
+        for acc, cols in zip(last_accs, pieces):
             product(acc[:], v_mx[last], cols)
-        y_pairs.append(keep.tile([P, 2, NQ], F32, name="y_high", tag="v_grouped%d" % last, align_bytes=64))
+        y_pairs.append(keep.tile([P, 2, NQ], F32, name="y_high"))
         add_residual(2, accs[2][:], whole)
         nc.sync.dma_start(out=y_rows[:, 2, :], in_=y_pairs[1][:, 0, :])
-        for acc, cols in zip(last_accs, halves):
+        for acc, cols in zip(last_accs, pieces):
             add_residual(last, acc[:], cols)
         nc.sync.dma_start(out=y_rows[:, last, :], in_=y_pairs[1][:, 1, :])
         round_pair(nc.scalar.copy, 1, slice(0, QUARTER))

@@ -20,6 +20,7 @@ NQ = 512
 HALF = NQ // 2
 QUARTER = NQ // 4
 W_SPLIT = 320
+Y_SPLIT = 192
 FLOPS = 2 * 512 * 512 * 512
 
 
@@ -140,11 +141,12 @@ def tile_attend_plo_wsumres_f_srt_kernel(tc, vT, wT, rs, offs, out_0, out_1, out
         y_pairs = [keep.tile([P, 2, NQ], F32, name="y_low")]
         y_grouped = keep.tile([P, NQ, PACK], BF16, name="y_grouped", tag="gathered%d" % last, align_bytes=64)
         nc.gpsimd.tensor_tensor(y_pairs[0][:, 0, halves[0]], acc0_low[:], rs_sb[:, 0, halves[0]], ADD)
+        add_residual(1, accs[1][:, halves[0]], halves[0])
         add_residual(0, accs[0][:, halves[1]], halves[1])
-        add_residual(1, accs[1][:], whole)
+        add_residual(1, accs[1][:, halves[1]], halves[1])
         nc.sync.dma_start(out=y_rows[:, 0:2, :], in_=y_pairs[0][:])
-        for cols in halves:
-            round_pair(nc.scalar.copy, 0, cols)
+        round_pair(nc.vector.tensor_copy, 0, slice(0, Y_SPLIT))
+        round_pair(nc.scalar.copy, 0, slice(Y_SPLIT, NQ))
         v_mx.append(quantise_values(last, v_grouped[last], "v_codes_last"))
         pieces = [slice(0, QUARTER), slice(QUARTER, HALF), halves[1]]
         last_accs = [psum.tile([P, c.stop - c.start], F32, name="acc_last%d" % i) for i, c in enumerate(pieces)]

@@ -21,6 +21,7 @@ HALF = NQ // 2
 QUARTER = NQ // 4
 W_SPLIT = 320
 Y_SPLIT = 192
+LAST_SHARE = 96
 FLOPS = 2 * 512 * 512 * 512
 
 
@@ -160,7 +161,8 @@ def tile_attend_plo_wsumres_f_srt_kernel(tc, vT, wT, rs, offs, out_0, out_1, out
         nc.sync.dma_start(out=y_rows[:, last, :], in_=y_pairs[1][:, 1, :])
         round_pair(nc.scalar.copy, 1, slice(0, QUARTER))
         round_pair(nc.vector.tensor_copy, 1, slice(QUARTER, HALF))
-        round_pair(nc.vector.tensor_copy, 1, halves[1])
+        round_pair(nc.vector.tensor_copy, 1, slice(HALF, NQ - LAST_SHARE))
+        round_pair(nc.scalar.copy, 1, slice(NQ - LAST_SHARE, NQ))
         for cols in halves:
             nc.vector.quantize_mx(
                 out=y_codes[:, cols].bitcast(FP8X4),

@@ -169,10 +169,9 @@ def tile_attend_plo_wsumres_f_srt_kernel(tc, vT, wT, rs, offs, out_0, out_1, out
                 scales=y_scales[:, cols],
                 in_=y_grouped[:, cols, :].rearrange("p q u -> p (q u)"),
             )
-            nc.sync.dma_start(out=words_out[:, cols], in_=y_codes[:, cols].bitcast(I32))
+            nc.scalar.dma_start(out=words_out[:, cols], in_=y_codes[:, cols].bitcast(I32))
         for quad in range(4):
-            queue = nc.scalar if quad % 2 == 0 else nc.sync
-            queue.dma_start(
+            nc.sync.dma_start(
                 out=scales_out[4 * quad : 4 * quad + 4, :],
                 in_=y_scales[32 * quad : 32 * quad + 4, :].bitcast(I32),
             )

@@ -11,6 +11,7 @@ U16 = mybir.dt.uint16
 U8 = mybir.dt.uint8
 FP8X4 = mybir.dt.float8_e4m3fn_x4
 ADD = mybir.AluOpType.add
+COPY = mybir.ActivationFunctionType.Copy
 
 P = 128
 PACK = 4
@@ -19,8 +20,9 @@ TOKENS = 2048
 NQ = 512
 HALF = NQ // 2
 QUARTER = NQ // 4
+GATHER_SPLIT = 288
 W_SPLIT = 320
-Y_SPLIT = 192
+Y_SPLIT = 160
 LAST_SHARE = 96
 FLOPS = 2 * 512 * 512 * 512
 
@@ -33,6 +35,9 @@ def tile_attend_plo_wsumres_f_srt_kernel(tc, vT, wT, rs, offs, out_0, out_1, out
     y_rows = out_0.rearrange("(m u) q -> m u q", u=PACK)
     words_out = out_1[0].rearrange("p q u -> p (q u)").bitcast(I32)
     scales_out = out_2[0].bitcast(I32)
+    last = PACK - 1
+    whole = slice(0, NQ)
+    halves = [slice(0, HALF), slice(HALF, NQ)]
 
     with ExitStack() as ctx:
         keep = ctx.enter_context(tc.tile_pool(name="keep", bufs=1))
@@ -42,16 +47,15 @@ def tile_attend_plo_wsumres_f_srt_kernel(tc, vT, wT, rs, offs, out_0, out_1, out
         v_first = keep.tile([P, 2, TOKENS], F32, name="v_first", tag="v_raw1", align_bytes=64)
         v_raw = {u: keep.tile([P, TOKENS], F32, name="v_raw%d" % u, tag="v_raw%d" % u, align_bytes=64) for u in (2, 3)}
         w_raw = keep.tile([P, PACK, NQ], F32, name="w_raw", tag="w_raw", align_bytes=64)
-        rs_sb = keep.tile([P, PACK, NQ], F32, name="rs_sb")
+        rs_sb = [keep.tile([P, NQ], F32, name="rs%d" % u) for u in range(PACK)]
 
         nc.sync.dma_start(out=v_first[:], in_=v_rows[:, 0:2, :])
         nc.sync.dma_start(offsets[:], offs)
-        last = PACK - 1
         nc.sync.dma_start(out=v_raw[2][:], in_=v_rows[:, 2, :])
         nc.sync.dma_start(out=w_raw[:], in_=w_rows)
         nc.sync.dma_start(out=v_raw[last][:], in_=v_rows[:, last, :])
-        for planes in (slice(0, 2), slice(2, 4)):
-            nc.sync.dma_start(out=rs_sb[:, planes, :], in_=rs_rows[:, planes, :])
+        for u in range(PACK):
+            nc.sync.dma_start(out=rs_sb[u][:], in_=rs_rows[:, u, :])
 
         identity = keep.tile([P, P], F32, name="identity")
         make_identity(nc, identity[:])
@@ -62,17 +66,23 @@ def tile_attend_plo_wsumres_f_srt_kernel(tc, vT, wT, rs, offs, out_0, out_1, out
         y_codes = keep.tile([P, NQ], U32, name="y_codes", align_bytes=64)
         y_scales = keep.tile([P, NQ], U8, name="y_scales", align_bytes=64)
 
-        def gather_and_turn(u):
+        def gather(u):
             gathered = keep.tile([P, SLOTS], BF16, name="gathered%d" % u, tag="gathered%d" % u, align_bytes=64)
             pairs = gathered[:].bitcast(F32)
             if u == 1:
                 dealt = gathered[:].rearrange("p (h w e) -> p w h e", h=2, e=2)
                 nc.vector.tensor_copy(dealt, v_first[:, 1, :].indirect(offsets[:]))
-                words = [pairs[:, h * P : (h + 1) * P] for h in range(2)]
-            else:
+                return [pairs[:, h * P : (h + 1) * P] for h in range(2)]
+            if u < last:
                 window = v_first[:].rearrange("p u t -> p (u t)") if u == 0 else v_raw[u][:]
                 nc.vector.tensor_copy(gathered[:], window.indirect(offsets[:]))
-                words = [pairs[:, h : 2 * P : 2] for h in range(2)]
+            else:
+                cut = GATHER_SPLIT // 16
+                nc.vector.tensor_copy(gathered[:, :GATHER_SPLIT], v_raw[u][:].indirect(offsets[:, :cut]))
+                nc.scalar.activation(gathered[:, GATHER_SPLIT:], v_raw[u][:].indirect(offsets[:, cut:]), COPY)
+            return [pairs[:, h : 2 * P : 2] for h in range(2)]
+
+        def turn(u, words):
             turned = psum.tile([P, 2, P], F32, name="turned%d" % (u % 2))
             for h in range(2):
                 nc.tensor.transpose(turned[:, h, :], words[h], identity[:])
@@ -101,7 +111,7 @@ def tile_attend_plo_wsumres_f_srt_kernel(tc, vT, wT, rs, offs, out_0, out_1, out
             )
 
         def add_residual(u, acc, cols):
-            nc.vector.tensor_tensor(y_pairs[u // 2][:, u % 2, cols], acc, rs_sb[:, u, cols], ADD)
+            nc.vector.tensor_tensor(y_pairs[u // 2][:, u % 2, cols], acc, rs_sb[u][:, cols], ADD)
 
         def round_weights(copy, cols):
             copy(
@@ -115,14 +125,12 @@ def tile_attend_plo_wsumres_f_srt_kernel(tc, vT, wT, rs, offs, out_0, out_1, out
                 in_=y_pairs[pair][:, :, cols].rearrange("p u q -> p q u"),
             )
 
-        whole = slice(0, NQ)
-        halves = [slice(0, HALF), slice(HALF, NQ)]
-
-        v_grouped = [gather_and_turn(0), gather_and_turn(1)]
+        v_grouped = [turn(u, gather(u)) for u in (0, 1)]
         v_mx = [quantise_values(0, v_grouped[0], "v_raw1")]
-        v_grouped.append(gather_and_turn(2))
+        v_grouped.append(turn(2, gather(2)))
         v_mx.append(quantise_values(1, v_grouped[1], "v_raw2"))
-        round_weights(nc.vector.tensor_copy, slice(0, W_SPLIT))
+        round_weights(nc.vector.tensor_copy, slice(0, HALF))
+        round_weights(nc.vector.tensor_copy, slice(HALF, W_SPLIT))
         round_weights(nc.scalar.copy, slice(W_SPLIT, NQ))
         for cols in halves:
             nc.vector.quantize_mx(
@@ -132,23 +140,21 @@ def tile_attend_plo_wsumres_f_srt_kernel(tc, vT, wT, rs, offs, out_0, out_1, out
             )
         v_mx.append(quantise_values(2, v_grouped[2], "w_raw"))
         accs = [psum.tile([P, NQ], F32, name="acc%d" % u) for u in range(last)]
-        for planes in ((0, 1), (2,)):
-            for cols in halves:
-                for u in planes:
-                    product(accs[u][:, cols], v_mx[u], cols)
-        acc0_low = keep.tile([P, HALF], F32, name="acc0_low")
-        nc.scalar.copy(out=acc0_low[:], in_=accs[0][:, halves[0]])
-        v_grouped.append(gather_and_turn(last))
+        for cols in halves:
+            for u in (0, 1):
+                product(accs[u][:, cols], v_mx[u], cols)
+        product(accs[2][:], v_mx[2], whole)
+
+        last_grouped = turn(last, gather(last))
         y_pairs = [keep.tile([P, 2, NQ], F32, name="y_low")]
-        y_grouped = keep.tile([P, NQ, PACK], BF16, name="y_grouped", tag="gathered%d" % last, align_bytes=64)
-        nc.gpsimd.tensor_tensor(y_pairs[0][:, 0, halves[0]], acc0_low[:], rs_sb[:, 0, halves[0]], ADD)
-        add_residual(1, accs[1][:, halves[0]], halves[0])
-        add_residual(0, accs[0][:, halves[1]], halves[1])
-        add_residual(1, accs[1][:, halves[1]], halves[1])
+        y_grouped = keep.tile([P, NQ, PACK], BF16, name="y_grouped", align_bytes=64)
+        add_residual(0, accs[0][:], whole)
+        for cols in reversed(halves):
+            add_residual(1, accs[1][:, cols], cols)
         nc.sync.dma_start(out=y_rows[:, 0:2, :], in_=y_pairs[0][:])
-        round_pair(nc.vector.tensor_copy, 0, slice(0, Y_SPLIT))
-        round_pair(nc.scalar.copy, 0, slice(Y_SPLIT, NQ))
-        v_mx.append(quantise_values(last, v_grouped[last], "v_codes_last"))
+        round_pair(nc.vector.tensor_copy, 0, slice(NQ - Y_SPLIT, NQ))
+        round_pair(nc.scalar.copy, 0, slice(0, NQ - Y_SPLIT))
+        v_mx.append(quantise_values(last, last_grouped, "v_codes_last"))
         pieces = [slice(0, QUARTER), slice(QUARTER, HALF), halves[1]]
         last_accs = [psum.tile([P, c.stop - c.start], F32, name="acc_last%d" % i) for i, c in enumerate(pieces)]
         for acc, cols in zip(last_accs, pieces):

@@ -86,7 +86,8 @@ def tile_attend_plo_wsumres_f_srt_kernel(tc, vT, wT, rs, offs, out_0, out_1, out
             turned = psum.tile([P, 2, P], F32, name="turned%d" % (u % 2))
             for h in range(2):
                 nc.tensor.transpose(turned[:, h, :], words[h], identity[:])
-            grouped = keep.tile([P, P, PACK], BF16, name="v_grouped%d" % u, tag="v_grouped%d" % u, align_bytes=64)
+            tag = "w_raw" if u == 2 else "v_grouped%d" % u
+            grouped = keep.tile([P, P, PACK], BF16, name="v_grouped%d" % u, tag=tag, align_bytes=64)
             nc.scalar.copy(out=grouped[:].bitcast(F32), in_=turned[:].rearrange("p h m -> p m h"))
             return grouped
 
@@ -127,7 +128,7 @@ def tile_attend_plo_wsumres_f_srt_kernel(tc, vT, wT, rs, offs, out_0, out_1, out
 
         v_grouped = [turn(u, gather(u)) for u in (0, 1)]
         v_mx = [quantise_values(0, v_grouped[0], "v_raw1")]
-        v_grouped.append(turn(2, gather(2)))
+        words2 = gather(2)
         v_mx.append(quantise_values(1, v_grouped[1], "v_raw2"))
         round_weights(nc.vector.tensor_copy, slice(0, HALF))
         round_weights(nc.vector.tensor_copy, slice(HALF, W_SPLIT))
@@ -138,19 +139,22 @@ def tile_attend_plo_wsumres_f_srt_kernel(tc, vT, wT, rs, offs, out_0, out_1, out
                 scales=w_scales[:, cols],
                 in_=w_grouped[:, cols, :].rearrange("p q t -> p (q t)"),
             )
-        v_mx.append(quantise_values(2, v_grouped[2], "w_raw"))
-        accs = [psum.tile([P, NQ], F32, name="acc%d" % u) for u in range(last)]
+        accs = [psum.tile([P, NQ], F32, name="acc%d" % u, tag="acc%d" % u) for u in (0, 1)]
         for cols in halves:
             for u in (0, 1):
                 product(accs[u][:, cols], v_mx[u], cols)
-        product(accs[2][:], v_mx[2], whole)
+        v_mx.append(quantise_values(2, turn(2, words2), "v_codes2"))
 
         last_grouped = turn(last, gather(last))
         y_pairs = [keep.tile([P, 2, NQ], F32, name="y_low")]
         y_grouped = keep.tile([P, NQ, PACK], BF16, name="y_grouped", align_bytes=64)
         add_residual(0, accs[0][:], whole)
+        acc2_low = psum.tile([P, HALF], F32, name="acc2_low", tag="acc0")
+        product(acc2_low[:], v_mx[2], halves[0])
         for cols in reversed(halves):
             add_residual(1, accs[1][:, cols], cols)
+        acc2_high = psum.tile([P, HALF], F32, name="acc2_high", tag="acc1")
+        product(acc2_high[:], v_mx[2], halves[1])
         nc.sync.dma_start(out=y_rows[:, 0:2, :], in_=y_pairs[0][:])
         round_pair(nc.vector.tensor_copy, 0, slice(NQ - Y_SPLIT, NQ))
         round_pair(nc.scalar.copy, 0, slice(0, NQ - Y_SPLIT))
@@ -160,7 +164,8 @@ def tile_attend_plo_wsumres_f_srt_kernel(tc, vT, wT, rs, offs, out_0, out_1, out
         for acc, cols in zip(last_accs, pieces):
             product(acc[:], v_mx[last], cols)
         y_pairs.append(keep.tile([P, 2, NQ], F32, name="y_high"))
-        add_residual(2, accs[2][:], whole)
+        add_residual(2, acc2_low[:], halves[0])
+        add_residual(2, acc2_high[:], halves[1])
         nc.sync.dma_start(out=y_rows[:, 2, :], in_=y_pairs[1][:, 0, :])
         for acc, cols in zip(last_accs, pieces):
             add_residual(last, acc[:], cols)

@@ -22,7 +22,7 @@ HALF = NQ // 2
 QUARTER = NQ // 4
 GATHER_SPLIT = 288
 W_SPLIT = 320
-Y_SPLIT = 160
+Y_SPLIT = 128
 LAST_SHARE = 96
 FLOPS = 2 * 512 * 512 * 512
 
@@ -47,7 +47,7 @@ def tile_attend_plo_wsumres_f_srt_kernel(tc, vT, wT, rs, offs, out_0, out_1, out
         v_first = keep.tile([P, 2, TOKENS], F32, name="v_first", tag="v_raw1", align_bytes=64)
         v_raw = {u: keep.tile([P, TOKENS], F32, name="v_raw%d" % u, tag="v_raw%d" % u, align_bytes=64) for u in (2, 3)}
         w_raw = keep.tile([P, PACK, NQ], F32, name="w_raw", tag="w_raw", align_bytes=64)
-        rs_sb = [keep.tile([P, NQ], F32, name="rs%d" % u) for u in range(PACK)]
+        rs_sb = [keep.tile([P, NQ], F32, name="rs%d" % u, tag="rs%d" % u, align_bytes=64) for u in range(PACK)]
 
         nc.sync.dma_start(out=v_first[:], in_=v_rows[:, 0:2, :])
         nc.sync.dma_start(offsets[:], offs)
@@ -55,7 +55,8 @@ def tile_attend_plo_wsumres_f_srt_kernel(tc, vT, wT, rs, offs, out_0, out_1, out
         nc.sync.dma_start(out=w_raw[:], in_=w_rows)
         nc.sync.dma_start(out=v_raw[last][:], in_=v_rows[:, last, :])
         for u in range(PACK):
-            nc.sync.dma_start(out=rs_sb[u][:], in_=rs_rows[:, u, :])
+            for cols in halves if u < 2 else [whole]:
+                nc.sync.dma_start(out=rs_sb[u][:, cols], in_=rs_rows[:, u, cols])
 
         identity = keep.tile([P, P], F32, name="identity")
         make_identity(nc, identity[:])
@@ -148,25 +149,27 @@ def tile_attend_plo_wsumres_f_srt_kernel(tc, vT, wT, rs, offs, out_0, out_1, out
         last_grouped = turn(last, gather(last))
         y_pairs = [keep.tile([P, 2, NQ], F32, name="y_low")]
         y_grouped = keep.tile([P, NQ, PACK], BF16, name="y_grouped", align_bytes=64)
-        add_residual(0, accs[0][:], whole)
+        for cols in halves:
+            add_residual(0, accs[0][:, cols], cols)
+            nc.sync.dma_start(out=y_rows[:, 0, cols], in_=y_pairs[0][:, 0, cols])
         acc2_low = psum.tile([P, HALF], F32, name="acc2_low", tag="acc0")
         product(acc2_low[:], v_mx[2], halves[0])
-        for cols in reversed(halves):
+        for cols in halves:
             add_residual(1, accs[1][:, cols], cols)
+            nc.sync.dma_start(out=y_rows[:, 1, cols], in_=y_pairs[0][:, 1, cols])
         acc2_high = psum.tile([P, HALF], F32, name="acc2_high", tag="acc1")
         product(acc2_high[:], v_mx[2], halves[1])
-        nc.sync.dma_start(out=y_rows[:, 0:2, :], in_=y_pairs[0][:])
         round_pair(nc.vector.tensor_copy, 0, slice(NQ - Y_SPLIT, NQ))
         round_pair(nc.scalar.copy, 0, slice(0, NQ - Y_SPLIT))
-        v_mx.append(quantise_values(last, last_grouped, "v_codes_last"))
+        v_mx.append(quantise_values(last, last_grouped, "rs1"))
         pieces = [slice(0, QUARTER), slice(QUARTER, HALF), halves[1]]
         last_accs = [psum.tile([P, c.stop - c.start], F32, name="acc_last%d" % i) for i, c in enumerate(pieces)]
         for acc, cols in zip(last_accs, pieces):
             product(acc[:], v_mx[last], cols)
         y_pairs.append(keep.tile([P, 2, NQ], F32, name="y_high"))
-        add_residual(2, acc2_low[:], halves[0])
-        add_residual(2, acc2_high[:], halves[1])
-        nc.sync.dma_start(out=y_rows[:, 2, :], in_=y_pairs[1][:, 0, :])
+        for acc, cols in zip((acc2_low, acc2_high), halves):
+            add_residual(2, acc[:], cols)
+            nc.sync.dma_start(out=y_rows[:, 2, cols], in_=y_pairs[1][:, 0, cols])
         for acc, cols in zip(last_accs, pieces):
             add_residual(last, acc[:], cols)
         nc.sync.dma_start(out=y_rows[:, last, :], in_=y_pairs[1][:, 1, :])

@@ -11,6 +11,7 @@ U16 = mybir.dt.uint16
 U8 = mybir.dt.uint8
 FP8X4 = mybir.dt.float8_e4m3fn_x4
 ADD = mybir.AluOpType.add
+MULT = mybir.AluOpType.mult
 COPY = mybir.ActivationFunctionType.Copy
 
 P = 128
@@ -20,10 +21,8 @@ TOKENS = 2048
 NQ = 512
 HALF = NQ // 2
 QUARTER = NQ // 4
-GATHER_SPLIT = 288
+GATHER_SPLIT = 320
 W_SPLIT = 320
-Y_SPLIT = 128
-LAST_SHARE = 96
 FLOPS = 2 * 512 * 512 * 512
 
 
@@ -38,6 +37,7 @@ def tile_attend_plo_wsumres_f_srt_kernel(tc, vT, wT, rs, offs, out_0, out_1, out
     last = PACK - 1
     whole = slice(0, NQ)
     halves = [slice(0, HALF), slice(HALF, NQ)]
+    quarters = [slice(first, first + QUARTER) for first in range(0, NQ, QUARTER)]
 
     with ExitStack() as ctx:
         keep = ctx.enter_context(tc.tile_pool(name="keep", bufs=1))
@@ -67,6 +67,9 @@ def tile_attend_plo_wsumres_f_srt_kernel(tc, vT, wT, rs, offs, out_0, out_1, out
         y_codes = keep.tile([P, NQ], U32, name="y_codes", align_bytes=64)
         y_scales = keep.tile([P, NQ], U8, name="y_scales", align_bytes=64)
 
+        def feature_parts(u):
+            return [slice(0, P // 2), slice(P // 2, P)] if u == last else [slice(0, P)]
+
         def gather(u):
             gathered = keep.tile([P, SLOTS], BF16, name="gathered%d" % u, tag="gathered%d" % u, align_bytes=64)
             pairs = gathered[:].bitcast(F32)
@@ -89,15 +92,19 @@ def tile_attend_plo_wsumres_f_srt_kernel(tc, vT, wT, rs, offs, out_0, out_1, out
                 nc.tensor.transpose(turned[:, h, :], words[h], identity[:])
             tag = "w_raw" if u == 2 else "v_grouped%d" % u
             grouped = keep.tile([P, P, PACK], BF16, name="v_grouped%d" % u, tag=tag, align_bytes=64)
-            nc.scalar.copy(out=grouped[:].bitcast(F32), in_=turned[:].rearrange("p h m -> p m h"))
+            for part in feature_parts(u):
+                nc.scalar.copy(out=grouped[:, part, :].bitcast(F32), in_=turned[:, :, part].rearrange("p h m -> p m h"))
             return grouped
 
         def quantise_values(u, grouped, codes_tag):
             codes = keep.tile([P, P], U32, name="v_codes%d" % u, tag=codes_tag, align_bytes=64)
             scales = keep.tile([P, P], U8, name="v_scales%d" % u, align_bytes=64)
-            nc.vector.quantize_mx(
-                out=codes[:].bitcast(FP8X4), scales=scales[:], in_=grouped[:].rearrange("p m t -> p (m t)")
-            )
+            for part in feature_parts(u):
+                nc.vector.quantize_mx(
+                    out=codes[:, part].bitcast(FP8X4),
+                    scales=scales[:, part],
+                    in_=grouped[:, part, :].rearrange("p m t -> p (m t)"),
+                )
             return codes, scales
 
         def product(acc, values, cols):
@@ -121,9 +128,23 @@ def tile_attend_plo_wsumres_f_srt_kernel(tc, vT, wT, rs, offs, out_0, out_1, out
                 in_=w_raw[:, :, cols].rearrange("p t (c i) -> p c t i", i=4),
             )
 
+        def rounded(cols):
+            part, first = divmod(cols.start, NQ - QUARTER)
+            return y_grouped[part][:, first : first + cols.stop - cols.start, :]
+
+        def quantise_result(cols):
+            nc.vector.quantize_mx(
+                out=y_codes[:, cols].bitcast(FP8X4),
+                scales=y_scales[:, cols],
+                in_=rounded(cols).rearrange("p q u -> p (q u)"),
+            )
+
+        def gpsimd_round(out, in_):
+            nc.gpsimd.tensor_scalar(out, in_, 1.0, 0.0, MULT, ADD)
+
         def round_pair(copy, pair, cols):
             copy(
-                out=y_grouped[:, cols, 2 * pair : 2 * pair + 2],
+                out=rounded(cols)[:, :, 2 * pair : 2 * pair + 2],
                 in_=y_pairs[pair][:, :, cols].rearrange("p u q -> p q u"),
             )
 
@@ -148,7 +169,7 @@ def tile_attend_plo_wsumres_f_srt_kernel(tc, vT, wT, rs, offs, out_0, out_1, out
 
         last_grouped = turn(last, gather(last))
         y_pairs = [keep.tile([P, 2, NQ], F32, name="y_low")]
-        y_grouped = keep.tile([P, NQ, PACK], BF16, name="y_grouped", align_bytes=64)
+        y_grouped = [keep.tile([P, NQ - QUARTER, PACK], BF16, name="y_grouped0", align_bytes=64)]
         for cols in halves:
             add_residual(0, accs[0][:, cols], cols)
             nc.sync.dma_start(out=y_rows[:, 0, cols], in_=y_pairs[0][:, 0, cols])
@@ -159,9 +180,12 @@ def tile_attend_plo_wsumres_f_srt_kernel(tc, vT, wT, rs, offs, out_0, out_1, out
             nc.sync.dma_start(out=y_rows[:, 1, cols], in_=y_pairs[0][:, 1, cols])
         acc2_high = psum.tile([P, HALF], F32, name="acc2_high", tag="acc1")
         product(acc2_high[:], v_mx[2], halves[1])
-        round_pair(nc.vector.tensor_copy, 0, slice(NQ - Y_SPLIT, NQ))
-        round_pair(nc.scalar.copy, 0, slice(0, NQ - Y_SPLIT))
+        round_pair(nc.scalar.copy, 0, slice(0, NQ - QUARTER))
         v_mx.append(quantise_values(last, last_grouped, "rs1"))
+        y_grouped.append(
+            keep.tile([P, QUARTER, PACK], BF16, name="y_grouped1", tag="v_grouped%d" % last, align_bytes=64)
+        )
+        round_pair(gpsimd_round, 0, quarters[3])
         pieces = [slice(0, QUARTER), slice(QUARTER, HALF), halves[1]]
         last_accs = [psum.tile([P, c.stop - c.start], F32, name="acc_last%d" % i) for i, c in enumerate(pieces)]
         for acc, cols in zip(last_accs, pieces):
@@ -173,17 +197,13 @@ def tile_attend_plo_wsumres_f_srt_kernel(tc, vT, wT, rs, offs, out_0, out_1, out
         for acc, cols in zip(last_accs, pieces):
             add_residual(last, acc[:], cols)
         nc.sync.dma_start(out=y_rows[:, last, :], in_=y_pairs[1][:, 1, :])
-        round_pair(nc.scalar.copy, 1, slice(0, QUARTER))
-        round_pair(nc.vector.tensor_copy, 1, slice(QUARTER, HALF))
-        round_pair(nc.vector.tensor_copy, 1, slice(HALF, NQ - LAST_SHARE))
-        round_pair(nc.scalar.copy, 1, slice(NQ - LAST_SHARE, NQ))
-        for cols in halves:
-            nc.vector.quantize_mx(
-                out=y_codes[:, cols].bitcast(FP8X4),
-                scales=y_scales[:, cols],
-                in_=y_grouped[:, cols, :].rearrange("p q u -> p (q u)"),
-            )
-            nc.scalar.dma_start(out=words_out[:, cols], in_=y_codes[:, cols].bitcast(I32))
+        for cols, copy in zip(quarters, (nc.scalar.copy, nc.vector.tensor_copy, nc.vector.tensor_copy, nc.scalar.copy)):
+            round_pair(copy, 1, cols)
+        quantise_result(halves[0])
+        nc.scalar.dma_start(out=words_out[:, halves[0]], in_=y_codes[:, halves[0]].bitcast(I32))
+        for cols in quarters[2:]:
+            quantise_result(cols)
+        nc.scalar.dma_start(out=words_out[:, halves[1]], in_=y_codes[:, halves[1]].bitcast(I32))
         for quad in range(4):
             nc.sync.dma_start(
                 out=scales_out[4 * quad : 4 * quad + 4, :],

@@ -162,10 +162,11 @@ def tile_attend_plo_wsumres_f_srt_kernel(tc, vT, wT, rs, offs, out_0, out_1, out
                 in_=w_grouped[:, cols, :].rearrange("p q t -> p (q t)"),
             )
         accs = [psum.tile([P, NQ], F32, name="acc%d" % u, tag="acc%d" % u) for u in (0, 1)]
-        for cols in halves:
-            for u in (0, 1):
-                product(accs[u][:, cols], v_mx[u], cols)
+        for u in (0, 1):
+            product(accs[u][:], v_mx[u], whole)
         v_mx.append(quantise_values(2, turn(2, words2), "v_codes2"))
+        acc2_low = psum.tile([P, HALF], F32, name="acc2_low")
+        product(acc2_low[:], v_mx[2], halves[0])
 
         last_grouped = turn(last, gather(last))
         y_pairs = [keep.tile([P, 2, NQ], F32, name="y_low")]
@@ -173,13 +174,11 @@ def tile_attend_plo_wsumres_f_srt_kernel(tc, vT, wT, rs, offs, out_0, out_1, out
         for cols in halves:
             add_residual(0, accs[0][:, cols], cols)
             nc.sync.dma_start(out=y_rows[:, 0, cols], in_=y_pairs[0][:, 0, cols])
-        acc2_low = psum.tile([P, HALF], F32, name="acc2_low", tag="acc0")
-        product(acc2_low[:], v_mx[2], halves[0])
+        acc2_high = psum.tile([P, HALF], F32, name="acc2_high", tag="acc0")
+        product(acc2_high[:], v_mx[2], halves[1])
         for cols in halves:
             add_residual(1, accs[1][:, cols], cols)
             nc.sync.dma_start(out=y_rows[:, 1, cols], in_=y_pairs[0][:, 1, cols])
-        acc2_high = psum.tile([P, HALF], F32, name="acc2_high", tag="acc1")
-        product(acc2_high[:], v_mx[2], halves[1])
         round_pair(nc.scalar.copy, 0, slice(0, NQ - QUARTER))
         v_mx.append(quantise_values(last, last_grouped, "rs1"))
         y_grouped.append(

@@ -23,6 +23,8 @@ HALF = NQ // 2
 QUARTER = NQ // 4
 GATHER_SPLIT = 320
 W_SPLIT = 320
+DMA_ALIGN = 256
+MX_ALIGN = 64
 FLOPS = 2 * 512 * 512 * 512
 
 
@@ -44,10 +46,13 @@ def tile_attend_plo_wsumres_f_srt_kernel(tc, vT, wT, rs, offs, out_0, out_1, out
         psum = ctx.enter_context(tc.psum_pool(name="psum", bufs=1))
 
         offsets = keep.tile([P, SLOTS // 16], U16, name="offsets")
-        v_first = keep.tile([P, 2, TOKENS], F32, name="v_first", tag="v_raw1", align_bytes=64)
-        v_raw = {u: keep.tile([P, TOKENS], F32, name="v_raw%d" % u, tag="v_raw%d" % u, align_bytes=64) for u in (2, 3)}
-        w_raw = keep.tile([P, PACK, NQ], F32, name="w_raw", tag="w_raw", align_bytes=64)
-        rs_sb = [keep.tile([P, NQ], F32, name="rs%d" % u, tag="rs%d" % u, align_bytes=64) for u in range(PACK)]
+        v_first = keep.tile([P, 2, TOKENS], F32, name="v_first", tag="v_raw1", align_bytes=DMA_ALIGN)
+        v_raw = {
+            u: keep.tile([P, TOKENS], F32, name="v_raw%d" % u, tag="v_raw%d" % u, align_bytes=DMA_ALIGN) for u in (2, 3)
+        }
+        w_raw = keep.tile([P, PACK, NQ], F32, name="w_raw", tag="w_raw", align_bytes=DMA_ALIGN)
+        rs_sb = [keep.tile([P, NQ], F32, name="rs%d" % u, tag="rs%d" % u, align_bytes=DMA_ALIGN) for u in range(PACK)]
+        y_pairs = [keep.tile([P, 2, NQ], F32, name="y_pair%d" % pair, align_bytes=DMA_ALIGN) for pair in range(2)]
 
         nc.sync.dma_start(out=v_first[:], in_=v_rows[:, 0:2, :])
         nc.sync.dma_start(offsets[:], offs)
@@ -61,17 +66,17 @@ def tile_attend_plo_wsumres_f_srt_kernel(tc, vT, wT, rs, offs, out_0, out_1, out
         identity = keep.tile([P, P], F32, name="identity")
         make_identity(nc, identity[:])
 
-        w_grouped = keep.tile([P, NQ, PACK], BF16, name="w_grouped", tag="gathered%d" % last, align_bytes=64)
-        w_codes = keep.tile([P, NQ], U32, name="w_codes", align_bytes=64)
-        w_scales = keep.tile([P, NQ], U8, name="w_scales", align_bytes=64)
-        y_codes = keep.tile([P, NQ], U32, name="y_codes", align_bytes=64)
-        y_scales = keep.tile([P, NQ], U8, name="y_scales", align_bytes=64)
+        w_grouped = keep.tile([P, NQ, PACK], BF16, name="w_grouped", tag="gathered%d" % last, align_bytes=MX_ALIGN)
+        w_codes = keep.tile([P, NQ], U32, name="w_codes", align_bytes=MX_ALIGN)
+        w_scales = keep.tile([P, NQ], U8, name="w_scales", align_bytes=MX_ALIGN)
+        y_codes = keep.tile([P, NQ], U32, name="y_codes", align_bytes=DMA_ALIGN)
+        y_scales = keep.tile([P, NQ], U8, name="y_scales", align_bytes=DMA_ALIGN)
 
         def feature_parts(u):
             return [slice(0, P // 2), slice(P // 2, P)] if u == last else [slice(0, P)]
 
         def gather(u):
-            gathered = keep.tile([P, SLOTS], BF16, name="gathered%d" % u, tag="gathered%d" % u, align_bytes=64)
+            gathered = keep.tile([P, SLOTS], BF16, name="gathered%d" % u, tag="gathered%d" % u, align_bytes=MX_ALIGN)
             pairs = gathered[:].bitcast(F32)
             if u == 1:
                 dealt = gathered[:].rearrange("p (h w e) -> p w h e", h=2, e=2)
@@ -90,15 +95,15 @@ def tile_attend_plo_wsumres_f_srt_kernel(tc, vT, wT, rs, offs, out_0, out_1, out
             turned = psum.tile([P, 2, P], F32, name="turned%d" % (u % 2))
             for h in range(2):
                 nc.tensor.transpose(turned[:, h, :], words[h], identity[:])
-            tag = "w_raw" if u == 2 else "v_grouped%d" % u
-            grouped = keep.tile([P, P, PACK], BF16, name="v_grouped%d" % u, tag=tag, align_bytes=64)
+            tag, align = ("w_raw", DMA_ALIGN) if u == 2 else ("v_grouped%d" % u, MX_ALIGN)
+            grouped = keep.tile([P, P, PACK], BF16, name="v_grouped%d" % u, tag=tag, align_bytes=align)
             for part in feature_parts(u):
                 nc.scalar.copy(out=grouped[:, part, :].bitcast(F32), in_=turned[:, :, part].rearrange("p h m -> p m h"))
             return grouped
 
         def quantise_values(u, grouped, codes_tag):
-            codes = keep.tile([P, P], U32, name="v_codes%d" % u, tag=codes_tag, align_bytes=64)
-            scales = keep.tile([P, P], U8, name="v_scales%d" % u, align_bytes=64)
+            codes = keep.tile([P, P], U32, name="v_codes%d" % u, tag=codes_tag, align_bytes=MX_ALIGN if u == 2 else DMA_ALIGN)
+            scales = keep.tile([P, P], U8, name="v_scales%d" % u, align_bytes=MX_ALIGN)
             for part in feature_parts(u):
                 nc.vector.quantize_mx(
                     out=codes[:, part].bitcast(FP8X4),
@@ -169,8 +174,7 @@ def tile_attend_plo_wsumres_f_srt_kernel(tc, vT, wT, rs, offs, out_0, out_1, out
         product(acc2_low[:], v_mx[2], halves[0])
 
         last_grouped = turn(last, gather(last))
-        y_pairs = [keep.tile([P, 2, NQ], F32, name="y_low")]
-        y_grouped = [keep.tile([P, NQ - QUARTER, PACK], BF16, name="y_grouped0", align_bytes=64)]
+        y_grouped = [keep.tile([P, NQ - QUARTER, PACK], BF16, name="y_grouped0", align_bytes=MX_ALIGN)]
         for cols in halves:
             add_residual(0, accs[0][:, cols], cols)
             nc.sync.dma_start(out=y_rows[:, 0, cols], in_=y_pairs[0][:, 0, cols])
@@ -182,14 +186,13 @@ def tile_attend_plo_wsumres_f_srt_kernel(tc, vT, wT, rs, offs, out_0, out_1, out
         round_pair(nc.scalar.copy, 0, slice(0, NQ - QUARTER))
         v_mx.append(quantise_values(last, last_grouped, "rs1"))
         y_grouped.append(
-            keep.tile([P, QUARTER, PACK], BF16, name="y_grouped1", tag="v_grouped%d" % last, align_bytes=64)
+            keep.tile([P, QUARTER, PACK], BF16, name="y_grouped1", tag="v_grouped%d" % last, align_bytes=MX_ALIGN)
         )
         round_pair(gpsimd_round, 0, quarters[3])
         pieces = [slice(0, QUARTER), slice(QUARTER, HALF), halves[1]]
         last_accs = [psum.tile([P, c.stop - c.start], F32, name="acc_last%d" % i) for i, c in enumerate(pieces)]
         for acc, cols in zip(last_accs, pieces):
             product(acc[:], v_mx[last], cols)
-        y_pairs.append(keep.tile([P, 2, NQ], F32, name="y_high"))
         for acc, cols in zip((acc2_low, acc2_high), halves):
             add_residual(2, acc[:], cols)
             nc.sync.dma_start(out=y_rows[:, 2, cols], in_=y_pairs[1][:, 0, cols])

@@ -22,7 +22,8 @@ NQ = 512
 HALF = NQ // 2
 QUARTER = NQ // 4
 GATHER_SPLIT = 320
-W_SPLIT = 320
+W_SPLIT = 160
+LATE_SPLIT = 192
 DMA_ALIGN = 256
 MX_ALIGN = 64
 FLOPS = 2 * 512 * 512 * 512
@@ -37,12 +38,12 @@ def tile_attend_plo_wsumres_f_srt_kernel(tc, vT, wT, rs, offs, out_0, out_1, out
     words_out = out_1[0].rearrange("p q u -> p (q u)").bitcast(I32)
     scales_out = out_2[0].bitcast(I32)
     last = PACK - 1
-    whole = slice(0, NQ)
     halves = [slice(0, HALF), slice(HALF, NQ)]
     quarters = [slice(first, first + QUARTER) for first in range(0, NQ, QUARTER)]
 
     with ExitStack() as ctx:
         keep = ctx.enter_context(tc.tile_pool(name="keep", bufs=1))
+        late = ctx.enter_context(tc.tile_pool(name="late", bufs=1))
         psum = ctx.enter_context(tc.psum_pool(name="psum", bufs=1))
 
         offsets = keep.tile([P, SLOTS // 16], U16, name="offsets")
@@ -50,33 +51,39 @@ def tile_attend_plo_wsumres_f_srt_kernel(tc, vT, wT, rs, offs, out_0, out_1, out
         v_raw = {
             u: keep.tile([P, TOKENS], F32, name="v_raw%d" % u, tag="v_raw%d" % u, align_bytes=DMA_ALIGN) for u in (2, 3)
         }
-        w_raw = keep.tile([P, PACK, NQ], F32, name="w_raw", tag="w_raw", align_bytes=DMA_ALIGN)
-        rs_sb = [keep.tile([P, NQ], F32, name="rs%d" % u, tag="rs%d" % u, align_bytes=DMA_ALIGN) for u in range(PACK)]
-        y_pairs = [keep.tile([P, 2, NQ], F32, name="y_pair%d" % pair, align_bytes=DMA_ALIGN) for pair in range(2)]
+        w_raw = [
+            keep.tile([P, PACK, HALF], F32, name="w_raw0", tag="w_raw0", align_bytes=DMA_ALIGN),
+            late.tile([P, PACK, HALF], F32, name="w_raw1", offset=3840, align_bytes=DMA_ALIGN),
+        ]
+        rs_first = [
+            keep.tile([P, 2, HALF], F32, name="rs_first%d" % h, tag="rs_first%d" % h, align_bytes=DMA_ALIGN)
+            for h in range(2)
+        ]
+        rs_sb = {u: keep.tile([P, NQ], F32, name="rs%d" % u, align_bytes=DMA_ALIGN) for u in (2, 3)}
 
         nc.sync.dma_start(out=v_first[:], in_=v_rows[:, 0:2, :])
         nc.sync.dma_start(offsets[:], offs)
         nc.sync.dma_start(out=v_raw[2][:], in_=v_rows[:, 2, :])
-        nc.sync.dma_start(out=w_raw[:], in_=w_rows)
+        nc.sync.dma_start(out=w_raw[0][:], in_=w_rows[:, :, halves[0]])
         nc.sync.dma_start(out=v_raw[last][:], in_=v_rows[:, last, :])
-        for u in range(PACK):
-            for cols in halves if u < 2 else [whole]:
-                nc.sync.dma_start(out=rs_sb[u][:, cols], in_=rs_rows[:, u, cols])
+        nc.sync.dma_start(out=w_raw[1][:], in_=w_rows[:, :, halves[1]])
+        nc.sync.dma_start(out=rs_first[0][:], in_=rs_rows[:, 0:2, halves[0]])
+        nc.sync.dma_start(out=rs_sb[2][:, halves[0]], in_=rs_rows[:, 2, halves[0]])
+        for u in range(2):
+            nc.sync.dma_start(out=rs_first[1][:, u, :], in_=rs_rows[:, u, halves[1]])
+        nc.sync.dma_start(out=rs_sb[2][:, halves[1]], in_=rs_rows[:, 2, halves[1]])
+        nc.sync.dma_start(out=rs_sb[last][:], in_=rs_rows[:, last, :])
 
         identity = keep.tile([P, P], F32, name="identity")
         make_identity(nc, identity[:])
 
-        w_grouped = keep.tile([P, NQ, PACK], BF16, name="w_grouped", tag="gathered%d" % last, align_bytes=MX_ALIGN)
         w_codes = keep.tile([P, NQ], U32, name="w_codes", align_bytes=MX_ALIGN)
         w_scales = keep.tile([P, NQ], U8, name="w_scales", align_bytes=MX_ALIGN)
         y_codes = keep.tile([P, NQ], U32, name="y_codes", align_bytes=DMA_ALIGN)
         y_scales = keep.tile([P, NQ], U8, name="y_scales", align_bytes=DMA_ALIGN)
 
-        def feature_parts(u):
-            return [slice(0, P // 2), slice(P // 2, P)] if u == last else [slice(0, P)]
-
-        def gather(u):
-            gathered = keep.tile([P, SLOTS], BF16, name="gathered%d" % u, tag="gathered%d" % u, align_bytes=MX_ALIGN)
+        def gather(u, tag):
+            gathered = keep.tile([P, SLOTS], BF16, name="gathered%d" % u, tag=tag, align_bytes=MX_ALIGN)
             pairs = gathered[:].bitcast(F32)
             if u == 1:
                 dealt = gathered[:].rearrange("p (h w e) -> p w h e", h=2, e=2)
@@ -91,25 +98,19 @@ def tile_attend_plo_wsumres_f_srt_kernel(tc, vT, wT, rs, offs, out_0, out_1, out
                 nc.scalar.activation(gathered[:, GATHER_SPLIT:], v_raw[u][:].indirect(offsets[:, cut:]), COPY)
             return [pairs[:, h : 2 * P : 2] for h in range(2)]
 
-        def turn(u, words):
+        def turn(u, words, grouped):
             turned = psum.tile([P, 2, P], F32, name="turned%d" % (u % 2))
             for h in range(2):
                 nc.tensor.transpose(turned[:, h, :], words[h], identity[:])
-            tag, align = ("w_raw", DMA_ALIGN) if u == 2 else ("v_grouped%d" % u, MX_ALIGN)
-            grouped = keep.tile([P, P, PACK], BF16, name="v_grouped%d" % u, tag=tag, align_bytes=align)
-            for part in feature_parts(u):
-                nc.scalar.copy(out=grouped[:, part, :].bitcast(F32), in_=turned[:, :, part].rearrange("p h m -> p m h"))
+            nc.scalar.copy(out=grouped[:].bitcast(F32), in_=turned[:].rearrange("p h m -> p m h"))
             return grouped
 
-        def quantise_values(u, grouped, codes_tag):
-            codes = keep.tile([P, P], U32, name="v_codes%d" % u, tag=codes_tag, align_bytes=MX_ALIGN if u == 2 else DMA_ALIGN)
+        def quantise_values(u, grouped, codes_tag, align):
+            codes = keep.tile([P, P], U32, name="v_codes%d" % u, tag=codes_tag, align_bytes=align)
             scales = keep.tile([P, P], U8, name="v_scales%d" % u, align_bytes=MX_ALIGN)
-            for part in feature_parts(u):
-                nc.vector.quantize_mx(
-                    out=codes[:, part].bitcast(FP8X4),
-                    scales=scales[:, part],
-                    in_=grouped[:, part, :].rearrange("p m t -> p (m t)"),
-                )
+            nc.vector.quantize_mx(
+                out=codes[:].bitcast(FP8X4), scales=scales[:], in_=grouped[:].rearrange("p m t -> p (m t)")
+            )
             return codes, scales
 
         def product(acc, values, cols):
@@ -125,12 +126,20 @@ def tile_attend_plo_wsumres_f_srt_kernel(tc, vT, wT, rs, offs, out_0, out_1, out
             )
 
         def add_residual(u, acc, cols):
-            nc.vector.tensor_tensor(y_pairs[u // 2][:, u % 2, cols], acc, rs_sb[u][:, cols], ADD)
+            nc.vector.tensor_tensor(y_pairs[1][:, u % 2, cols], acc, rs_sb[u][:, cols], ADD)
 
-        def round_weights(copy, cols):
+        def round_weights(copy, grouped, h, cols):
             copy(
-                out=w_grouped[:, cols, :].rearrange("p (c i) t -> p c t i", i=4),
-                in_=w_raw[:, :, cols].rearrange("p t (c i) -> p c t i", i=4),
+                out=grouped[:, cols, :].rearrange("p (c i) t -> p c t i", i=4),
+                in_=w_raw[h][:, :, cols].rearrange("p t (c i) -> p c t i", i=4),
+            )
+
+        def quantise_weights(grouped, h, cols):
+            at = slice(h * HALF + cols.start, h * HALF + cols.stop)
+            nc.vector.quantize_mx(
+                out=w_codes[:, at].bitcast(FP8X4),
+                scales=w_scales[:, at],
+                in_=grouped[:, cols, :].rearrange("p q t -> p (q t)"),
             )
 
         def rounded(cols):
@@ -153,49 +162,70 @@ def tile_attend_plo_wsumres_f_srt_kernel(tc, vT, wT, rs, offs, out_0, out_1, out
                 in_=y_pairs[pair][:, :, cols].rearrange("p u q -> p q u"),
             )
 
-        v_grouped = [turn(u, gather(u)) for u in (0, 1)]
-        v_mx = [quantise_values(0, v_grouped[0], "v_raw1")]
-        words2 = gather(2)
-        v_mx.append(quantise_values(1, v_grouped[1], "v_raw2"))
-        round_weights(nc.vector.tensor_copy, slice(0, HALF))
-        round_weights(nc.vector.tensor_copy, slice(HALF, W_SPLIT))
-        round_weights(nc.scalar.copy, slice(W_SPLIT, NQ))
-        for cols in halves:
-            nc.vector.quantize_mx(
-                out=w_codes[:, cols].bitcast(FP8X4),
-                scales=w_scales[:, cols],
-                in_=w_grouped[:, cols, :].rearrange("p q t -> p (q t)"),
-            )
-        accs = [psum.tile([P, NQ], F32, name="acc%d" % u, tag="acc%d" % u) for u in (0, 1)]
-        for u in (0, 1):
-            product(accs[u][:], v_mx[u], whole)
-        v_mx.append(quantise_values(2, turn(2, words2), "v_codes2"))
-        acc2_low = psum.tile([P, HALF], F32, name="acc2_low")
-        product(acc2_low[:], v_mx[2], halves[0])
+        def first_pair(h, acc):
+            for u in range(2):
+                nc.vector.tensor_tensor(y_pairs[0][:, u, halves[h]], acc[u], rs_first[h][:, u, :], ADD)
+                nc.sync.dma_start(out=y_rows[:, u, halves[h]], in_=y_pairs[0][:, u, halves[h]])
 
-        last_grouped = turn(last, gather(last))
+        v_grouped = [
+            turn(u, gather(u, "gathered%d" % u), keep.tile([P, P, PACK], BF16, name="v_grouped%d" % u, align_bytes=MX_ALIGN))
+            for u in (0, 1)
+        ]
+        v_mx = [quantise_values(0, v_grouped[0], "v_raw1", DMA_ALIGN)]
+        words2 = gather(2, "gathered2")
+        v_mx.append(quantise_values(1, v_grouped[1], "v_raw2", DMA_ALIGN))
+        w_grouped0 = keep.tile([P, HALF, PACK], BF16, name="w_grouped0", tag="gathered3", align_bytes=MX_ALIGN)
+        round_weights(nc.vector.tensor_copy, w_grouped0, 0, slice(0, W_SPLIT))
+        round_weights(nc.scalar.copy, w_grouped0, 0, slice(W_SPLIT, HALF))
+        quantise_weights(w_grouped0, 0, slice(0, HALF))
+        acc_low = psum.tile([P, 2, HALF], F32, name="acc_low")
+        for u in range(2):
+            product(acc_low[:, u, :], v_mx[u], halves[0])
+        grouped2 = keep.tile([P, P, PACK], BF16, name="v_grouped2", tag="w_raw0", align_bytes=DMA_ALIGN)
+        v_mx.append(quantise_values(2, turn(2, words2, grouped2), "v_codes2", MX_ALIGN))
+        acc2 = [psum.tile([P, HALF], F32, name="acc2_low", tag="turned0")]
+        product(acc2[0][:], v_mx[2], halves[0])
+
+        words3 = gather(last, "gathered3")
+        w_grouped1 = keep.tile([P, HALF, PACK], BF16, name="w_grouped1", tag="gathered2", align_bytes=MX_ALIGN)
+        round_weights(nc.vector.tensor_copy, w_grouped1, 1, slice(0, QUARTER))
+        round_weights(nc.vector.tensor_copy, w_grouped1, 1, slice(QUARTER, LATE_SPLIT))
+        round_weights(nc.scalar.copy, w_grouped1, 1, slice(LATE_SPLIT, HALF))
+        sums2_low = late.tile([P, HALF], F32, name="sums2_low", offset=4864, align_bytes=DMA_ALIGN)
+        nc.scalar.copy(out=sums2_low[:], in_=acc2[0][:])
+        last_grouped = late.tile([P, P, PACK], BF16, name="v_grouped3", offset=3840, align_bytes=DMA_ALIGN)
+        turn(last, words3, last_grouped)
+        for cols in quarters[:2]:
+            quantise_weights(w_grouped1, 1, cols)
+        acc_high = [psum.tile([P, HALF], F32, name="acc_high%d" % u) for u in range(2)]
+        for u in range(2):
+            product(acc_high[u][:], v_mx[u], halves[1])
+        acc2.append(psum.tile([P, HALF], F32, name="acc2_high"))
+        product(acc2[1][:], v_mx[2], halves[1])
+        y_pairs = [
+            late.tile([P, 2, NQ], F32, name="y_pair0", offset=5888, align_bytes=DMA_ALIGN),
+        ]
         y_grouped = [keep.tile([P, NQ - QUARTER, PACK], BF16, name="y_grouped0", align_bytes=MX_ALIGN)]
-        for cols in halves:
-            add_residual(0, accs[0][:, cols], cols)
-            nc.sync.dma_start(out=y_rows[:, 0, cols], in_=y_pairs[0][:, 0, cols])
-        acc2_high = psum.tile([P, HALF], F32, name="acc2_high", tag="acc0")
-        product(acc2_high[:], v_mx[2], halves[1])
-        for cols in halves:
-            add_residual(1, accs[1][:, cols], cols)
-            nc.sync.dma_start(out=y_rows[:, 1, cols], in_=y_pairs[0][:, 1, cols])
-        round_pair(nc.scalar.copy, 0, slice(0, NQ - QUARTER))
-        v_mx.append(quantise_values(last, last_grouped, "rs1"))
-        y_grouped.append(
-            keep.tile([P, QUARTER, PACK], BF16, name="y_grouped1", tag="v_grouped%d" % last, align_bytes=MX_ALIGN)
-        )
+        nc.vector.tensor_tensor(y_pairs[0][:, :, halves[0]], acc_low[:], rs_first[0][:], ADD)
+        for u in range(2):
+            nc.sync.dma_start(out=y_rows[:, u, halves[0]], in_=y_pairs[0][:, u, halves[0]])
+        round_pair(nc.scalar.copy, 0, halves[0])
+        v_mx.append(quantise_values(last, last_grouped, "v_codes3", MX_ALIGN))
+        y_pairs.append(late.tile([P, 2, NQ], F32, name="y_pair1", offset=0, align_bytes=DMA_ALIGN))
+        nc.gpsimd.tensor_tensor(y_pairs[1][:, 0, halves[0]], sums2_low[:], rs_sb[2][:, halves[0]], ADD)
+        first_pair(1, [acc[:] for acc in acc_high])
+        round_pair(nc.scalar.copy, 0, quarters[2])
+        y_grouped.append(keep.tile([P, QUARTER, PACK], BF16, name="y_grouped1", align_bytes=MX_ALIGN))
         round_pair(gpsimd_round, 0, quarters[3])
         pieces = [slice(0, QUARTER), slice(QUARTER, HALF), halves[1]]
-        last_accs = [psum.tile([P, c.stop - c.start], F32, name="acc_last%d" % i) for i, c in enumerate(pieces)]
+        last_accs = [
+            psum.tile([P, c.stop - c.start], F32, name="acc_last%d" % i, tag=tag)
+            for i, (c, tag) in enumerate(zip(pieces, ("turned1", "acc_last1", "acc_last2")))
+        ]
         for acc, cols in zip(last_accs, pieces):
             product(acc[:], v_mx[last], cols)
-        for acc, cols in zip((acc2_low, acc2_high), halves):
-            add_residual(2, acc[:], cols)
-            nc.sync.dma_start(out=y_rows[:, 2, cols], in_=y_pairs[1][:, 0, cols])
+        add_residual(2, acc2[1][:], halves[1])
+        nc.sync.dma_start(out=y_rows[:, 2, :], in_=y_pairs[1][:, 0, :])
         for acc, cols in zip(last_accs, pieces):
             add_residual(last, acc[:], cols)
         nc.sync.dma_start(out=y_rows[:, last, :], in_=y_pairs[1][:, 1, :])

@@ -206,9 +206,7 @@ def tile_attend_plo_wsumres_f_srt_kernel(tc, vT, wT, rs, offs, out_0, out_1, out
             late.tile([P, 2, NQ], F32, name="y_pair0", offset=5888, align_bytes=DMA_ALIGN),
         ]
         y_grouped = [keep.tile([P, NQ - QUARTER, PACK], BF16, name="y_grouped0", align_bytes=MX_ALIGN)]
-        nc.vector.tensor_tensor(y_pairs[0][:, :, halves[0]], acc_low[:], rs_first[0][:], ADD)
-        for u in range(2):
-            nc.sync.dma_start(out=y_rows[:, u, halves[0]], in_=y_pairs[0][:, u, halves[0]])
+        first_pair(0, [acc_low[:, u, :] for u in range(2)])
         round_pair(nc.scalar.copy, 0, halves[0])
         v_mx.append(quantise_values(last, last_grouped, "v_codes3", MX_ALIGN))
         y_pairs.append(late.tile([P, 2, NQ], F32, name="y_pair1", offset=0, align_bytes=DMA_ALIGN))

from contextlib import ExitStack

import concourse.mybir as mybir
from concourse.masks import make_identity

F32 = mybir.dt.float32
BF16 = mybir.dt.bfloat16
I32 = mybir.dt.int32
U32 = mybir.dt.uint32
U16 = mybir.dt.uint16
U8 = mybir.dt.uint8
FP8X4 = mybir.dt.float8_e4m3fn_x4
ADD = mybir.AluOpType.add
MULT = mybir.AluOpType.mult
COPY = mybir.ActivationFunctionType.Copy

P = 128
PACK = 4
SLOTS = 512
TOKENS = 2048
NQ = 512
HALF = NQ // 2
QUARTER = NQ // 4
GATHER_SPLIT = 320
W_SPLIT = 160
LATE_SPLIT = 192
DMA_ALIGN = 256
MX_ALIGN = 64
FLOPS = 2 * 512 * 512 * 512


def tile_attend_plo_wsumres_f_srt_kernel(tc, vT, wT, rs, offs, out_0, out_1, out_2):
    nc = tc.nc
    v_rows = vT.rearrange("(m u) t -> m u t", u=PACK)
    w_rows = wT[0].rearrange("(p j) q -> p j q", j=PACK)
    rs_rows = rs[0].rearrange("(m u) q -> m u q", u=PACK)
    y_rows = out_0.rearrange("(m u) q -> m u q", u=PACK)
    words_out = out_1[0].rearrange("p q u -> p (q u)").bitcast(I32)
    scales_out = out_2[0].bitcast(I32)
    last = PACK - 1
    halves = [slice(0, HALF), slice(HALF, NQ)]
    quarters = [slice(first, first + QUARTER) for first in range(0, NQ, QUARTER)]

    with ExitStack() as ctx:
        keep = ctx.enter_context(tc.tile_pool(name="keep", bufs=1))
        late = ctx.enter_context(tc.tile_pool(name="late", bufs=1))
        psum = ctx.enter_context(tc.psum_pool(name="psum", bufs=1))

        offsets = keep.tile([P, SLOTS // 16], U16, name="offsets")
        v_first = keep.tile([P, 2, TOKENS], F32, name="v_first", tag="v_raw1", align_bytes=DMA_ALIGN)
        v_raw = {
            u: keep.tile([P, TOKENS], F32, name="v_raw%d" % u, tag="v_raw%d" % u, align_bytes=DMA_ALIGN) for u in (2, 3)
        }
        w_raw = [
            keep.tile([P, PACK, HALF], F32, name="w_raw0", tag="w_raw0", align_bytes=DMA_ALIGN),
            late.tile([P, PACK, HALF], F32, name="w_raw1", offset=3840, align_bytes=DMA_ALIGN),
        ]
        rs_first = [
            keep.tile([P, 2, HALF], F32, name="rs_first%d" % h, tag="rs_first%d" % h, align_bytes=DMA_ALIGN)
            for h in range(2)
        ]
        rs_sb = {u: keep.tile([P, NQ], F32, name="rs%d" % u, align_bytes=DMA_ALIGN) for u in (2, 3)}

        nc.sync.dma_start(out=v_first[:], in_=v_rows[:, 0:2, :])
        nc.sync.dma_start(offsets[:], offs)
        nc.sync.dma_start(out=v_raw[2][:], in_=v_rows[:, 2, :])
        nc.sync.dma_start(out=w_raw[0][:], in_=w_rows[:, :, halves[0]])
        nc.sync.dma_start(out=v_raw[last][:], in_=v_rows[:, last, :])
        nc.sync.dma_start(out=w_raw[1][:], in_=w_rows[:, :, halves[1]])
        nc.sync.dma_start(out=rs_first[0][:], in_=rs_rows[:, 0:2, halves[0]])
        nc.sync.dma_start(out=rs_sb[2][:, halves[0]], in_=rs_rows[:, 2, halves[0]])
        for u in range(2):
            nc.sync.dma_start(out=rs_first[1][:, u, :], in_=rs_rows[:, u, halves[1]])
        nc.sync.dma_start(out=rs_sb[2][:, halves[1]], in_=rs_rows[:, 2, halves[1]])
        nc.sync.dma_start(out=rs_sb[last][:], in_=rs_rows[:, last, :])

        identity = keep.tile([P, P], F32, name="identity")
        make_identity(nc, identity[:])

        w_codes = keep.tile([P, NQ], U32, name="w_codes", align_bytes=MX_ALIGN)
        w_scales = keep.tile([P, NQ], U8, name="w_scales", align_bytes=MX_ALIGN)
        y_codes = keep.tile([P, NQ], U32, name="y_codes", align_bytes=DMA_ALIGN)
        y_scales = keep.tile([P, NQ], U8, name="y_scales", align_bytes=DMA_ALIGN)

        def gather(u, tag):
            gathered = keep.tile([P, SLOTS], BF16, name="gathered%d" % u, tag=tag, align_bytes=MX_ALIGN)
            pairs = gathered[:].bitcast(F32)
            if u == 1:
                dealt = gathered[:].rearrange("p (h w e) -> p w h e", h=2, e=2)
                nc.vector.tensor_copy(dealt, v_first[:, 1, :].indirect(offsets[:]))
                return [pairs[:, h * P : (h + 1) * P] for h in range(2)]
            if u < last:
                window = v_first[:].rearrange("p u t -> p (u t)") if u == 0 else v_raw[u][:]
                nc.vector.tensor_copy(gathered[:], window.indirect(offsets[:]))
            else:
                cut = GATHER_SPLIT // 16
                nc.vector.tensor_copy(gathered[:, :GATHER_SPLIT], v_raw[u][:].indirect(offsets[:, :cut]))
                nc.scalar.activation(gathered[:, GATHER_SPLIT:], v_raw[u][:].indirect(offsets[:, cut:]), COPY)
            return [pairs[:, h : 2 * P : 2] for h in range(2)]

        def turn(u, words, grouped):
            turned = psum.tile([P, 2, P], F32, name="turned%d" % (u % 2))
            for h in range(2):
                nc.tensor.transpose(turned[:, h, :], words[h], identity[:])
            nc.scalar.copy(out=grouped[:].bitcast(F32), in_=turned[:].rearrange("p h m -> p m h"))
            return grouped

        def quantise_values(u, grouped, codes_tag, align):
            codes = keep.tile([P, P], U32, name="v_codes%d" % u, tag=codes_tag, align_bytes=align)
            scales = keep.tile([P, P], U8, name="v_scales%d" % u, align_bytes=MX_ALIGN)
            nc.vector.quantize_mx(
                out=codes[:].bitcast(FP8X4), scales=scales[:], in_=grouped[:].rearrange("p m t -> p (m t)")
            )
            return codes, scales

        def product(acc, values, cols):
            codes, scales = values
            nc.tensor.matmul_mx(
                out=acc,
                lhsT=codes[:].bitcast(FP8X4),
                lhsT_scale=scales[:],
                rhs=w_codes[:, cols].bitcast(FP8X4),
                rhs_scale=w_scales[:, cols],
                start=True,
                stop=True,
            )

        def add_residual(u, acc, cols):
            nc.vector.tensor_tensor(y_pairs[1][:, u % 2, cols], acc, rs_sb[u][:, cols], ADD)

        def round_weights(copy, grouped, h, cols):
            copy(
                out=grouped[:, cols, :].rearrange("p (c i) t -> p c t i", i=4),
                in_=w_raw[h][:, :, cols].rearrange("p t (c i) -> p c t i", i=4),
            )

        def quantise_weights(grouped, h, cols):
            at = slice(h * HALF + cols.start, h * HALF + cols.stop)
            nc.vector.quantize_mx(
                out=w_codes[:, at].bitcast(FP8X4),
                scales=w_scales[:, at],
                in_=grouped[:, cols, :].rearrange("p q t -> p (q t)"),
            )

        def rounded(cols):
            part, first = divmod(cols.start, NQ - QUARTER)
            return y_grouped[part][:, first : first + cols.stop - cols.start, :]

        def quantise_result(cols):
            nc.vector.quantize_mx(
                out=y_codes[:, cols].bitcast(FP8X4),
                scales=y_scales[:, cols],
                in_=rounded(cols).rearrange("p q u -> p (q u)"),
            )

        def gpsimd_round(out, in_):
            nc.gpsimd.tensor_scalar(out, in_, 1.0, 0.0, MULT, ADD)

        def round_pair(copy, pair, cols):
            copy(
                out=rounded(cols)[:, :, 2 * pair : 2 * pair + 2],
                in_=y_pairs[pair][:, :, cols].rearrange("p u q -> p q u"),
            )

        def first_pair(h, acc):
            for u in range(2):
                nc.vector.tensor_tensor(y_pairs[0][:, u, halves[h]], acc[u], rs_first[h][:, u, :], ADD)
                nc.sync.dma_start(out=y_rows[:, u, halves[h]], in_=y_pairs[0][:, u, halves[h]])

        v_grouped = [
            turn(u, gather(u, "gathered%d" % u), keep.tile([P, P, PACK], BF16, name="v_grouped%d" % u, align_bytes=MX_ALIGN))
            for u in (0, 1)
        ]
        v_mx = [quantise_values(0, v_grouped[0], "v_raw1", DMA_ALIGN)]
        words2 = gather(2, "gathered2")
        v_mx.append(quantise_values(1, v_grouped[1], "v_raw2", DMA_ALIGN))
        w_grouped0 = keep.tile([P, HALF, PACK], BF16, name="w_grouped0", tag="gathered3", align_bytes=MX_ALIGN)
        round_weights(nc.vector.tensor_copy, w_grouped0, 0, slice(0, W_SPLIT))
        round_weights(nc.scalar.copy, w_grouped0, 0, slice(W_SPLIT, HALF))
        quantise_weights(w_grouped0, 0, slice(0, HALF))
        acc_low = psum.tile([P, 2, HALF], F32, name="acc_low")
        for u in range(2):
            product(acc_low[:, u, :], v_mx[u], halves[0])
        grouped2 = keep.tile([P, P, PACK], BF16, name="v_grouped2", tag="w_raw0", align_bytes=DMA_ALIGN)
        v_mx.append(quantise_values(2, turn(2, words2, grouped2), "v_codes2", MX_ALIGN))
        acc2 = [psum.tile([P, HALF], F32, name="acc2_low", tag="turned0")]
        product(acc2[0][:], v_mx[2], halves[0])

        words3 = gather(last, "gathered3")
        w_grouped1 = keep.tile([P, HALF, PACK], BF16, name="w_grouped1", tag="gathered2", align_bytes=MX_ALIGN)
        round_weights(nc.vector.tensor_copy, w_grouped1, 1, slice(0, QUARTER))
        round_weights(nc.vector.tensor_copy, w_grouped1, 1, slice(QUARTER, LATE_SPLIT))
        round_weights(nc.scalar.copy, w_grouped1, 1, slice(LATE_SPLIT, HALF))
        sums2_low = late.tile([P, HALF], F32, name="sums2_low", offset=4864, align_bytes=DMA_ALIGN)
        nc.scalar.copy(out=sums2_low[:], in_=acc2[0][:])
        last_grouped = late.tile([P, P, PACK], BF16, name="v_grouped3", offset=3840, align_bytes=DMA_ALIGN)
        turn(last, words3, last_grouped)
        for cols in quarters[:2]:
            quantise_weights(w_grouped1, 1, cols)
        acc_high = [psum.tile([P, HALF], F32, name="acc_high%d" % u) for u in range(2)]
        for u in range(2):
            product(acc_high[u][:], v_mx[u], halves[1])
        acc2.append(psum.tile([P, HALF], F32, name="acc2_high"))
        product(acc2[1][:], v_mx[2], halves[1])
        y_pairs = [
            late.tile([P, 2, NQ], F32, name="y_pair0", offset=5888, align_bytes=DMA_ALIGN),
        ]
        y_grouped = [keep.tile([P, NQ - QUARTER, PACK], BF16, name="y_grouped0", align_bytes=MX_ALIGN)]
        first_pair(0, [acc_low[:, u, :] for u in range(2)])
        round_pair(nc.scalar.copy, 0, halves[0])
        v_mx.append(quantise_values(last, last_grouped, "v_codes3", MX_ALIGN))
        y_pairs.append(late.tile([P, 2, NQ], F32, name="y_pair1", offset=0, align_bytes=DMA_ALIGN))
        nc.gpsimd.tensor_tensor(y_pairs[1][:, 0, halves[0]], sums2_low[:], rs_sb[2][:, halves[0]], ADD)
        first_pair(1, [acc[:] for acc in acc_high])
        round_pair(nc.scalar.copy, 0, quarters[2])
        y_grouped.append(keep.tile([P, QUARTER, PACK], BF16, name="y_grouped1", align_bytes=MX_ALIGN))
        round_pair(gpsimd_round, 0, quarters[3])
        pieces = [slice(0, QUARTER), slice(QUARTER, HALF), halves[1]]
        last_accs = [
            psum.tile([P, c.stop - c.start], F32, name="acc_last%d" % i, tag=tag)
            for i, (c, tag) in enumerate(zip(pieces, ("turned1", "acc_last1", "acc_last2")))
        ]
        for acc, cols in zip(last_accs, pieces):
            product(acc[:], v_mx[last], cols)
        add_residual(2, acc2[1][:], halves[1])
        nc.sync.dma_start(out=y_rows[:, 2, :], in_=y_pairs[1][:, 0, :])
        for acc, cols in zip(last_accs, pieces):
            add_residual(last, acc[:], cols)
        nc.sync.dma_start(out=y_rows[:, last, :], in_=y_pairs[1][:, 1, :])
        for cols, copy in zip(quarters, (nc.scalar.copy, nc.vector.tensor_copy, nc.vector.tensor_copy, nc.scalar.copy)):
            round_pair(copy, 1, cols)
        quantise_result(halves[0])
        nc.scalar.dma_start(out=words_out[:, halves[0]], in_=y_codes[:, halves[0]].bitcast(I32))
        for cols in quarters[2:]:
            quantise_result(cols)
        nc.scalar.dma_start(out=words_out[:, halves[1]], in_=y_codes[:, halves[1]].bitcast(I32))
        for quad in range(4):
            nc.sync.dma_start(
                out=scales_out[4 * quad : 4 * quad + 4, :],
                in_=y_scales[32 * quad : 32 * quad + 4, :].bitcast(I32),
            )
